import numpy as np
import ml_dtypes


def mxq(x, axis, fmt="e4m3"):
    dtype, down = {"e4m3": (ml_dtypes.float8_e4m3fn, 7), "e5m2": (ml_dtypes.float8_e5m2, 14)}[fmt]
    v = np.moveaxis(np.asarray(x, np.float32).astype(ml_dtypes.bfloat16).astype(np.float64), axis, -1)
    blocks = v.reshape(v.shape[:-1] + (-1, 32))
    amax = np.abs(blocks).max(-1, keepdims=True)
    byte = np.maximum(np.where(amax > 0, np.frexp(amax)[1] - 1 + 127, 0) - down, 1)
    scale = np.exp2(byte - 127.0)
    codes = (blocks / scale).astype(np.float32).astype(dtype).astype(np.float64)
    return np.moveaxis((codes * scale).reshape(v.shape), -1, axis)


WIDE = False


def mx_kscale(k):
    if not WIDE:
        return np.ones(k)
    levels = np.array([10, -10, 5, -5, 0])
    if k % 512:
        return np.exp2(np.random.permutation(np.resize(levels, k // 32))).repeat(32)
    a = np.empty((k // 512, 16))
    for p in range(k // 512):
        a[p, :8] = np.random.permutation(np.resize(levels, 8))
        for g in range(8):
            far = levels[np.abs(levels - a[p, g]) >= 10]
            a[p, g + 8] = far[np.random.randint(len(far))]
    return np.exp2(a.ravel()).repeat(32)


BF16 = ml_dtypes.bfloat16


def bf(x):
    return np.asarray(x, np.float32).astype(BF16)


def f64(x):
    return np.asarray(x).astype(np.float64)


E2M1 = np.array([0.0, 0.5, 1.0, 1.5, 2.0, 3.0, 4.0, 6.0, -0.0, -0.5, -1.0, -1.5, -2.0, -3.0, -4.0, -6.0])


def pack_weight(w, fmt):
    k, n = w.shape
    w = f64(bf(w)).reshape(k // 32, 32, n)
    amax = np.abs(w).max(1)
    if fmt == "e4m3":
        byte = np.frexp(amax)[1] - 1 + 127 - 7
    else:
        mant, ex = np.frexp(amax / 6.0)
        byte = np.where(mant > 0.5, ex, ex - 1) + 127
    byte = np.clip(np.where(amax > 0, byte, 1), 1, 254)
    scaled = (w * np.exp2(127.0 - byte)[:, None, :]).reshape(k, n).astype(np.float32)
    by_word = np.ascontiguousarray(scaled.reshape(k // 512, 128, 4, n).transpose(0, 1, 3, 2))
    if fmt == "e4m3":
        words = by_word.astype(ml_dtypes.float8_e4m3fn).view(np.uint8)
    else:
        c = by_word.astype(ml_dtypes.float4_e2m1fn).view(np.uint8) & 0xF
        words = c[..., 0::2] | (c[..., 1::2] << 4)
    return np.ascontiguousarray(words), np.ascontiguousarray(byte.astype(np.uint8).reshape(k // 512, 16, n))


def unpack_weight(words, scales, fmt):
    g, p, n, _ = words.shape
    if fmt == "e4m3":
        vals = np.ascontiguousarray(words).view(ml_dtypes.float8_e4m3fn).astype(np.float64)
    else:
        nib = np.empty((g, p, n, 4), np.uint8)
        nib[..., 0::2] = words & 0xF
        nib[..., 1::2] = words >> 4
        vals = E2M1[nib]
    vals = vals * np.repeat(np.exp2(scales.astype(np.float64) - 127.0), 8, axis=1)[..., None]
    return vals.transpose(0, 1, 3, 2).reshape(g * 512, n)
def pack4(w):
    words, scales = pack_weight(w, "e2m1")
    return words.reshape(words.shape[0], 128, -1), scales


def unpack4(words, scales):
    return unpack_weight(words.reshape(words.shape[0], 128, -1, 2), scales, "e2m1")


def planes(Y):
    n, m = Y.shape
    b = f64(bf(Y)).reshape(n // 32, 32, m)
    amax = np.abs(b).max(1)
    byte = np.clip(np.where(amax > 0, np.frexp(amax)[1] - 1 + 127 - 7, 1), 1, 254)
    codes = (b * np.exp2(127.0 - byte)[:, None, :]).reshape(n, m).astype(np.float32).astype(ml_dtypes.float8_e4m3fn).view(np.uint8)
    words = codes.reshape(n // 512, 128, 4, m).transpose(0, 1, 3, 2)
    return np.ascontiguousarray(words), np.ascontiguousarray(byte.astype(np.uint8).reshape(n // 512, 16, m))


M, P, L, R, N = 1024, 1024, 512, 1024, 2048


def setup_inputs():
    s, r, t = mx_kscale(P), mx_kscale(R), mx_kscale(L)
    X = np.random.randn(P, M) * s[:, None]
    D = 1.5 * np.random.randn(P, L) * P ** -0.5 * L ** -0.25 * t[None, :] / s[:, None]
    spread = np.random.randn(L, R) * (2.0 / R) ** 0.5 * L ** -0.25 / t[:, None] / r[None, :]
    delays = np.random.rand(R)
    waves = np.cos(2.0 * np.pi * delays[:, None] * np.arange(N)[None, :]) * r[:, None]
    nsr = 0.1 * np.exp(3.0 * np.arange(L) / L + 0.3 * np.random.randn(L))
    front = np.exp(0.7 * np.random.randn(N))
    los = 0.4 * front * np.random.randn(N)
    agc = np.exp(0.3 * np.random.randn(M))
    x_words, x_scales = pack_weight(X, "e4m3")
    d_words, d_scales = pack4(D)
    return {"x_words": x_words, "x_scales": x_scales, "d_words": d_words, "d_scales": d_scales,
            "spread": bf(spread), "waves": bf(waves), "nsr": bf(nsr), "front": bf(front),
            "los": bf(los), "agc": bf(agc)}


def reference(x_words, x_scales, d_words, d_scales, spread, waves, nsr, front, los, agc):
    X = unpack_weight(x_words, x_scales, "e4m3")
    D = unpack4(d_words, d_scales)
    taps = X.T @ D
    shrunk = taps / (1.0 + f64(nsr)[None, :])
    C = (mxq(f64(spread), 1, "e4m3") @ mxq(f64(waves), 0, "e4m3")) * f64(front)[None, :]
    est = mxq(shrunk, 1, "e4m3") @ mxq(C, 0, "e4m3")
    y = (est + f64(los)[None, :]) * f64(agc)[:, None]
    words, scales = planes(y.T)
    return y, words, scales

@@ -1,0 +1,526 @@
+from contextlib import ExitStack
+
+import concourse.mybir as mybir
+from concourse.masks import make_identity
+
+M, PILOTS, L, R, N = 1024, 1024, 512, 1024, 2048
+FLOPS = 2 * (M * PILOTS * L + L * R * N + M * L * N)
+
+F32 = mybir.dt.float32
+BF16 = mybir.dt.bfloat16
+I32 = mybir.dt.int32
+U32 = mybir.dt.uint32
+U8 = mybir.dt.uint8
+FP8X4 = mybir.dt.float8_e4m3fn_x4
+FP4X4 = mybir.dt.float4_e2m1fn_x4
+ALU = mybir.AluOpType
+ACT = mybir.ActivationFunctionType
+
+P = 128
+PACK = 4
+K_PASS = 512
+WIDE = 512
+HALF = 256
+CHUNKS = N // WIDE
+SLOTS = 10
+MX_BANKS = 4
+TR_BANKS = 4
+
+
+def tile_delay_shrink_channel_k4_kernel(
+    tc, x_words, x_scales, d_words, d_scales, spread, waves, nsr, front, los, agc, out_0, out_1, out_2
+):
+    nc = tc.nc
+    with ExitStack() as ctx:
+        keep = ctx.enter_context(tc.tile_pool(name="keep", bufs=1))
+        work = ctx.enter_context(tc.tile_pool(name="work", bufs=1))
+        psum = ctx.enter_context(tc.psum_pool(name="psum", bufs=1))
+        ctx.enter_context(tc.manual_schedule())
+
+        def kept(name, shape, dtype):
+            return keep.tile(shape, dtype, name=name, align_bytes=64)
+
+        ident_f = kept("ident_f", [P, P], F32)
+        ident_b = kept("ident_b", [P, P], BF16)
+        front_col = kept("front_col", [P, CHUNKS, PACK], BF16)
+        los_col = kept("los_col", [P, CHUNKS, PACK], BF16)
+        nsr_rows = kept("nsr_rows", [P, P], BF16)
+        one_plus = kept("one_plus", [P, PACK], F32)
+        wiener = kept("wiener", [P, PACK], F32)
+        front_all = kept("front_all", [P, N], BF16)
+        agc_all = kept("agc_all", [P, M], BF16)
+        spread_raw = [kept("spread_raw%d" % i, [P, 2, R], BF16) for i in range(2)]
+        spread_bf = [kept("spread_bf%d" % k, [P, L * PACK], BF16) for k in range(2)]
+        spread_codes = [kept("spread_codes%d" % k, [P, L], U32) for k in range(2)]
+        spread_scales = [kept("spread_scales%d" % k, [P, L], U8) for k in range(2)]
+        d_raw = kept("d_raw", [P, 2, 2 * L], U8)
+        d_codes = kept("d_codes", [P, 2, 2 * L], U8)
+        ds_raw = kept("ds_raw", [P, 2, L], U8)
+        ds_plane = kept("ds_plane", [P, 2, L], U8)
+        x_codes = [kept("x_codes%d" % h, [P, 2, WIDE], U32) for h in range(2)]
+        xs_plane = kept("xs_plane", [P, 2, M], U8)
+        waves_raw = {}
+        waves_codes = {}
+        waves_scales = {}
+        for g in range(CHUNKS):
+            for k in range(2):
+                waves_raw[g, k] = kept("waves_raw%d%d" % (g, k), [P, PACK, WIDE], BF16)
+                waves_codes[g, k] = kept("waves_codes%d%d" % (g, k), [P, WIDE], U32)
+                waves_scales[g, k] = kept("waves_scales%d%d" % (g, k), [P, WIDE], U8)
+        taps_bf = [kept("taps_bf%d" % h, [P, PACK, WIDE], BF16) for h in range(2)]
+        shrunk_codes = [kept("shrunk_codes%d" % h, [P, WIDE], U32) for h in range(2)]
+        shrunk_scales = [kept("shrunk_scales%d" % h, [P, WIDE], U8) for h in range(2)]
+        c_bf = [kept("c_bf%d" % g, [P, WIDE * PACK], BF16) for g in range(CHUNKS)]
+        c_codes = [kept("c_codes%d" % g, [P, WIDE], U32) for g in range(CHUNKS)]
+        c_scales = [kept("c_scales%d" % g, [P, WIDE], U8) for g in range(CHUNKS)]
+        y_codes = {}
+        for g in range(CHUNKS):
+            for h in range(2):
+                y_codes[g, h] = kept("y_codes%d%d" % (g, h), [P, WIDE], U32)
+        y_scales = kept("y_scales", [P, M], U8)
+
+        count = {"mx": 0, "tr": 0, "yt": 0, "yo": 0, "filled": 0, "taken": 0}
+
+        def bank(kind, shape, dtype):
+            n_banks = MX_BANKS if kind == "mx" else TR_BANKS
+            tag = "%s%d" % (kind, count[kind] % n_banks)
+            count[kind] = count[kind] + 1
+            return psum.tile(shape, dtype, name=tag, tag=tag)
+
+        def load_waves(g, k):
+            src = waves[K_PASS * k : K_PASS * (k + 1), WIDE * g : WIDE * (g + 1)]
+            nc.sync.dma_start(out=waves_raw[g, k][:], in_=src.rearrange("(p j) n -> p j n", j=PACK))
+
+        def load_spread(i):
+            src = spread.rearrange("(a p) k -> p a k", p=P)
+            nc.sync.dma_start(out=spread_raw[i][:], in_=src[:, 2 * i : 2 * i + 2, :])
+
+        def load_x(h):
+            src = x_words.rearrange("g p m t -> p g (m t)")[:, :, 4 * WIDE * h : 4 * WIDE * (h + 1)]
+            nc.sync.dma_start(out=x_codes[h][:].bitcast(I32), in_=src.bitcast(I32))
+
+        def load_scale_rows(queue, plane, rows, q):
+            src = rows[:, 4 * q : 4 * q + 4, :].rearrange("g r n -> r g n")
+            queue.dma_start(out=plane[32 * q : 32 * q + 4, :, :].bitcast(I32), in_=src.bitcast(I32))
+
+        make_identity(nc, ident_f[:])
+        nc.vector.memset(ds_raw[:].bitcast(I32), 0)
+        nc.vector.memset(xs_plane[:].bitcast(I32), 0)
+        nc.vector.memset(nsr_rows[:], 0.0)
+        nc.vector.tensor_copy(out=ident_b[:], in_=ident_f[:])
+
+        load_spread(0)
+        load_waves(0, 0)
+        load_spread(1)
+        nc.sync.dma_start(out=d_raw[:].bitcast(I32), in_=d_words.rearrange("g p b -> p g b").bitcast(I32))
+        nc.scalar.dma_start(out=front_col[:], in_=front.rearrange("(g p t) -> p g t", g=CHUNKS, t=PACK))
+        for q in range(3):
+            load_scale_rows(nc.scalar, ds_raw, d_scales, q)
+        for q in range(1, 4):
+            load_scale_rows(nc.gpsimd, xs_plane, x_scales, q)
+        load_x(0)
+        load_waves(0, 1)
+        load_x(1)
+        load_waves(1, 0)
+        nc.scalar.dma_start(
+            out=nsr_rows[0:PACK, :].rearrange("s (q r) -> s q r", r=8),
+            in_=nsr.rearrange("(q s r) -> s q r", s=PACK, r=8),
+        )
+        load_scale_rows(nc.scalar, ds_raw, d_scales, 3)
+        load_scale_rows(nc.scalar, xs_plane, x_scales, 0)
+        nc.scalar.dma_start(out=los_col[:], in_=los.rearrange("(g p t) -> p g t", g=CHUNKS, t=PACK))
+        load_waves(1, 1)
+        nc.sync.dma_start(out=agc_all[:], in_=agc.partition_broadcast(P))
+        for g in range(2, CHUNKS):
+            for k in range(2):
+                load_waves(g, k)
+
+        free = ["slot%d" % i for i in range(SLOTS)]
+        staged = {}
+        made = set()
+
+        def interleave(engine, key, rows, gated=False):
+            tag = free[-1] if gated else free[0]
+            free.remove(tag)
+            tile = work.tile([P, HALF * PACK], BF16, name=tag, tag=tag, align_bytes=64)
+            staged[key] = (tag, tile)
+            if engine == "gpsimd":
+                nc.gpsimd.tensor_scalar(
+                    out=tile[:].rearrange("p (m t) -> p m t", t=PACK),
+                    in0=rows.rearrange("p t m -> p m t"),
+                    scalar1=1.0, scalar2=0.0, op0=ALU.mult, op1=ALU.add,
+                )
+            else:
+                dst = tile[:].rearrange("p (c i t) -> p c t i", i=4, t=PACK)
+                src = rows.rearrange("p t (c i) -> p c t i", i=4)
+                if engine == "vector":
+                    nc.vector.tensor_copy(out=dst, in_=src)
+                else:
+                    nc.scalar.copy(out=dst, in_=src)
+
+        def quantise(key, codes, scales):
+            tag, tile = staged[key]
+            nc.vector.quantize_mx(out=codes.bitcast(FP8X4), scales=scales, in_=tile[:])
+            free.append(tag)
+            made.add(key)
+
+        def half(x):
+            return slice(HALF * x, HALF * (x + 1))
+
+        def lay_waves(engine, g, k, x, gated=False):
+            interleave(engine, ("w", g, k, x), waves_raw[g, k][:, :, half(x)], gated)
+
+        def q_waves(g, k, x):
+            quantise(("w", g, k, x), waves_codes[g, k][:, half(x)], waves_scales[g, k][:, half(x)])
+            fill()
+
+        def lay_taps(engine, h, x, gated=False):
+            interleave(engine, ("s", h, x), taps_bf[h][:, :, half(x)], gated)
+
+        def q_taps(h, x):
+            quantise(("s", h, x), shrunk_codes[h][:, half(x)], shrunk_scales[h][:, half(x)])
+            fill()
+
+        y_t = {}
+
+        def lay_y(engine, g, h, x, gated=False):
+            interleave(engine, ("y", g, h, x), y_t[g, h][:, :, half(x)], gated)
+
+        def q_y(g, h, x):
+            cols = slice(WIDE * h + HALF * x, WIDE * h + HALF * (x + 1))
+            quantise(("y", g, h, x), y_codes[g, h][:, half(x)], y_scales[4 * g :, cols])
+
+        def store_codes(g, h):
+            dst = out_1[g].rearrange("p m t -> p (m t)")[:, 4 * WIDE * h : 4 * WIDE * (h + 1)]
+            nc.sync.dma_start(out=dst.bitcast(I32), in_=y_codes[g, h][:].bitcast(I32))
+
+        def store_scales(g0):
+            for q in range(4):
+                nc.sync.dma_start(
+                    out=out_2[g0 : g0 + 2, 4 * q : 4 * q + 4, :].bitcast(I32),
+                    in_=y_scales[32 * q + 4 * g0 : 32 * q + 4 * g0 + 8, :].bitcast(I32),
+                )
+
+        def q_c(g):
+            nc.vector.quantize_mx(out=c_codes[g][:].bitcast(FP8X4), scales=c_scales[g][:], in_=c_bf[g][:])
+            made.add(("c", g))
+            fill()
+
+        def mm_taps(acc, h, s):
+            for k in range(2):
+                nc.tensor.matmul_mx(
+                    out=acc[:],
+                    lhsT=d_codes[:, k, 2 * P * s : 2 * P * (s + 1)].bitcast(FP4X4),
+                    lhsT_scale=ds_plane[:, k, P * s : P * (s + 1)],
+                    rhs=x_codes[h][:, k, :].bitcast(FP8X4),
+                    rhs_scale=xs_plane[:, k, WIDE * h : WIDE * (h + 1)],
+                    start=(k == 0), stop=(k == 1),
+                )
+
+        def read_taps(acc, h, s):
+            nc.scalar.activation(out=taps_bf[h][:, s, :], in_=acc[:], func=ACT.Copy, scale=wiener[:, s : s + 1])
+
+        def mm_c(acc, g, b):
+            cols = slice(P * b, P * (b + 1))
+            for s in range(PACK):
+                for k in range(2):
+                    nc.tensor.matmul_mx(
+                        out=acc[:, P * s : P * (s + 1)],
+                        lhsT=spread_codes[k][:, P * s : P * (s + 1)].bitcast(FP8X4),
+                        lhsT_scale=spread_scales[k][:, P * s : P * (s + 1)],
+                        rhs=waves_codes[g, k][:, cols].bitcast(FP8X4),
+                        rhs_scale=waves_scales[g, k][:, cols],
+                        start=(k == 0), stop=(k == 1),
+                    )
+
+        def read_c(acc, g, b):
+            a = slice(32 * b, 32 * (b + 1))
+            dst = c_bf[g][:].rearrange("p (t a s) -> p t a s", t=PACK, s=PACK)[:, :, a, :]
+            gain = front_all[:, WIDE * g : WIDE * (g + 1)].rearrange("p (t a) -> p t a", t=PACK)[:, :, a]
+            nc.vector.tensor_tensor(
+                out=dst,
+                in0=acc[:].rearrange("p (s a t) -> p t a s", s=PACK, t=PACK),
+                in1=gain.unsqueeze(3).to_broadcast([P, PACK, 32, PACK]),
+                op=ALU.mult,
+            )
+
+        def mm_est(acc, g, h, t):
+            nc.tensor.matmul_mx(
+                out=acc[:],
+                lhsT=c_codes[g][:, P * t : P * (t + 1)].bitcast(FP8X4),
+                lhsT_scale=c_scales[g][:, P * t : P * (t + 1)],
+                rhs=shrunk_codes[h][:].bitcast(FP8X4),
+                rhs_scale=shrunk_scales[h][:],
+                start=True, stop=True,
+            )
+
+        def read_est(acc, g, h, t):
+            if t == 0:
+                tag = "y_t%d" % (count["yt"] % 4)
+                count["yt"] = count["yt"] + 1
+                y_t[g, h] = work.tile([P, PACK, WIDE], F32, name=tag, tag=tag, align_bytes=64)
+            nc.vector.scalar_tensor_tensor(
+                out=y_t[g, h][:, t, :], in0=acc[:], scalar=los_col[:, g, t : t + 1],
+                in1=agc_all[:, WIDE * h : WIDE * (h + 1)], op0=ALU.add, op1=ALU.mult,
+            )
+
+        def mm_est_half(acc, g, h, x, pair):
+            for e in range(2):
+                t = 2 * pair + e
+                nc.tensor.matmul_mx(
+                    out=acc[:, half(e)],
+                    lhsT=c_codes[g][:, P * t : P * (t + 1)].bitcast(FP8X4),
+                    lhsT_scale=c_scales[g][:, P * t : P * (t + 1)],
+                    rhs=shrunk_codes[h][:, half(x)].bitcast(FP8X4),
+                    rhs_scale=shrunk_scales[h][:, half(x)],
+                    start=True, stop=True,
+                )
+
+        def read_est_half(acc, g, h, x, pair):
+            if x == 0 and pair == 0:
+                tag = "y_t%d" % (count["yt"] % 4)
+                count["yt"] = count["yt"] + 1
+                y_t[g, h] = work.tile([P, PACK, WIDE], F32, name=tag, tag=tag, align_bytes=64)
+            for e in range(2):
+                t = 2 * pair + e
+                nc.vector.scalar_tensor_tensor(
+                    out=y_t[g, h][:, t, half(x)], in0=acc[:, half(e)], scalar=los_col[:, g, t : t + 1],
+                    in1=agc_all[:, WIDE * h + HALF * x : WIDE * h + HALF * (x + 1)], op0=ALU.add, op1=ALU.mult,
+                )
+
+        def needs_c(g, b):
+            return [("w", g, k, b // 2) for k in range(2)] + ["spread"]
+
+        def needs_est(g, h):
+            return [("c", g), ("s", h, 0), ("s", h, 1)]
+
+        def mm_front(acc, i):
+            view = acc[:].bitcast(BF16)
+            for c in range(8):
+                col = front_col[:, 2 * i + c // PACK, c % PACK : c % PACK + 1]
+                nc.tensor.transpose(view[:, P * c : P * (c + 1)], col.to_broadcast([P, P]), ident_b[:])
+
+        def read_front(acc, i):
+            dst = front_all[:, 1024 * i : 1024 * (i + 1)]
+            nc.scalar.copy(out=dst, in_=acc[:].bitcast(BF16))
+
+        def c_banks(g, banks):
+            return [(mm_c, read_c, (g, b), needs_c(g, b)) for b in banks]
+
+        def est_banks(g, h):
+            return [(mm_est, read_est, (g, h, t), needs_est(g, h)) for t in range(PACK)]
+
+        line = [(mm_front, read_front, (i,), []) for i in range(2)]
+        line.extend([(mm_taps, read_taps, (0, s), ["d"]) for s in range(PACK)])
+        line.extend(c_banks(0, range(4)))
+        for g in range(CHUNKS):
+            for h in range(2):
+                if (g, h) == (CHUNKS - 1, 1):
+                    for x in range(2):
+                        line.extend([(mm_est_half, read_est_half, (g, h, x, pair), needs_est(g, h)) for pair in range(2)])
+                else:
+                    line.extend(est_banks(g, h))
+                if g + 1 < CHUNKS:
+                    line.extend(c_banks(g + 1, range(2 * h, 2 * h + 2)))
+        held = {}
+
+        def fill():
+            while count["filled"] < min(len(line), count["taken"] + MX_BANKS):
+                matmuls, reader, args, needs = line[count["filled"]]
+                if not all(n in made for n in needs):
+                    return
+                acc = bank("mx", [P, WIDE], F32)
+                matmuls(acc, *args)
+                held[count["filled"]] = acc
+                count["filled"] = count["filled"] + 1
+
+        def take(n):
+            for step in range(n):
+                matmuls, reader, args, needs = line[count["taken"]]
+                reader(held[count["taken"]], *args)
+                count["taken"] = count["taken"] + 1
+                fill()
+
+        def turn_and_store(g, h, x):
+            tag = "y_out%d" % (count["yo"] % 6)
+            count["yo"] = count["yo"] + 1
+            y_out = work.tile([P, 2, WIDE], F32, name=tag, tag=tag, align_bytes=64)
+            turned = []
+            for j in range(2):
+                tr = bank("tr", [P, PACK, P], F32)
+                cols = slice(HALF * x + P * j, HALF * x + P * (j + 1))
+                for t in range(PACK):
+                    nc.tensor.transpose(tr[:, t, :], y_t[g, h][:, t, cols], ident_f[:])
+                turned.append(tr)
+            for j in range(2):
+                nc.scalar.copy(
+                    out=y_out[:, j, :].rearrange("p (a t) -> p a t", t=PACK),
+                    in_=turned[j][:].rearrange("p t a -> p a t"),
+                )
+            first = WIDE * h + HALF * x
+            rows = out_0[first : first + HALF, WIDE * g : WIDE * (g + 1)]
+            nc.sync.dma_start(out=rows.rearrange("(j p) n -> p j n", p=P), in_=y_out[:])
+
+        fill()
+        take(2)
+        lay_waves("vector", 0, 0, 0)
+        lay_waves("vector", 0, 0, 1)
+        q_waves(0, 0, 0)
+        q_waves(0, 0, 1)
+        for i in range(2):
+            for k in range(2):
+                tr = bank("tr", [P, 2, 2, P], F32)
+                for u in range(2):
+                    for a in range(2):
+                        words = spread_raw[i][:, a, :].bitcast(F32)
+                        nc.tensor.transpose(tr[:, u, a, :], words[:, 256 * k + u : 256 * (k + 1) : 2], ident_f[:])
+                dst = spread_bf[k][:].bitcast(F32).rearrange("p (s i q r u) -> p s i q r u", s=PACK, i=2, q=8, r=8)
+                nc.scalar.copy(
+                    out=dst[:, :, i, :, :, :],
+                    in_=tr[:].rearrange("p u a (c s r) -> p s (a c) r u", s=PACK, r=8),
+                )
+        for raw, laid in ((ds_raw, ds_plane), (d_raw, d_codes)):
+            nc.vector.tensor_copy(
+                out=laid[:].bitcast(I32).rearrange("p g (s q r) -> p g s q r", s=PACK, q=16),
+                in_=raw[:].bitcast(I32).rearrange("p g (q s r) -> p g s q r", s=PACK, q=16),
+            )
+        tr_nsr = bank("tr", [P, P], BF16)
+        nc.tensor.transpose(tr_nsr[:], nsr_rows[:], ident_b[:])
+        made.add("d")
+        fill()
+
+        def q_spread(k):
+            nc.vector.quantize_mx(out=spread_codes[k][:].bitcast(FP8X4), scales=spread_scales[k][:], in_=spread_bf[k][:])
+
+        nc.vector.tensor_scalar(out=one_plus[:], in0=tr_nsr[:, 0:PACK], scalar1=1.0, scalar2=None, op0=ALU.add)
+        q_spread(0)
+        nc.vector.reciprocal(out=wiener[:], in_=one_plus[:])
+        q_spread(1)
+        made.add("spread")
+        take(4)
+        lay_waves("vector", 0, 1, 0)
+        lay_waves("vector", 0, 1, 1)
+        q_waves(0, 1, 0)
+        q_waves(0, 1, 1)
+        second_taps = []
+
+        def second_taps_bank(s):
+            acc = bank("tr", [P, WIDE], F32)
+            mm_taps(acc, 1, s)
+            second_taps.append(acc)
+
+        lay_taps("gpsimd", 0, 0, gated=True)
+        lay_taps("gpsimd", 0, 1)
+        for s in range(PACK):
+            second_taps_bank(s)
+        lay_waves("scalar", 1, 0, 0)
+        lay_waves("scalar", 1, 1, 0)
+        take(4)
+        q_taps(0, 0)
+        q_c(0)
+        q_taps(0, 1)
+        q_waves(1, 0, 0)
+        q_waves(1, 1, 0)
+        for s in range(PACK):
+            read_taps(second_taps[s], 1, s)
+        lay_taps("scalar", 1, 0)
+        lay_taps("scalar", 1, 1)
+
+        lay_waves("gpsimd", 1, 0, 1, gated=True)
+        lay_waves("gpsimd", 1, 1, 1)
+        take(4)
+        turn_and_store(0, 0, 0)
+        turn_and_store(0, 0, 1)
+        lay_y("scalar", 0, 0, 0)
+        lay_y("scalar", 0, 0, 1)
+        take(2)
+        q_waves(1, 0, 1)
+        q_taps(1, 0)
+        q_taps(1, 1)
+        q_waves(1, 1, 1)
+        lay_waves("gpsimd", 2, 0, 0, gated=True)
+        lay_waves("gpsimd", 2, 1, 0)
+        take(4)
+        turn_and_store(0, 1, 0)
+        turn_and_store(0, 1, 1)
+        lay_y("scalar", 0, 1, 0)
+        lay_y("scalar", 0, 1, 1)
+        take(2)
+        q_waves(2, 0, 0)
+        q_c(1)
+        q_y(0, 0, 0)
+        q_y(0, 0, 1)
+        q_waves(2, 1, 0)
+        store_codes(0, 0)
+        lay_waves("gpsimd", 2, 0, 1, gated=True)
+        lay_waves("gpsimd", 2, 1, 1)
+        take(4)
+        turn_and_store(1, 0, 0)
+        turn_and_store(1, 0, 1)
+        lay_y("scalar", 1, 0, 0)
+        lay_y("scalar", 1, 0, 1)
+        take(2)
+        q_waves(2, 0, 1)
+        q_waves(2, 1, 1)
+        lay_waves("gpsimd", 3, 0, 0, gated=True)
+        lay_waves("gpsimd", 3, 1, 0)
+        take(4)
+        turn_and_store(1, 1, 0)
+        turn_and_store(1, 1, 1)
+        lay_y("scalar", 1, 1, 0)
+        lay_y("scalar", 1, 1, 1)
+        take(2)
+        q_waves(3, 0, 0)
+        q_c(2)
+        q_y(0, 1, 0)
+        q_y(0, 1, 1)
+        q_waves(3, 1, 0)
+        store_codes(0, 1)
+        lay_waves("gpsimd", 3, 0, 1, gated=True)
+        lay_waves("gpsimd", 3, 1, 1)
+        take(4)
+        turn_and_store(2, 0, 0)
+        turn_and_store(2, 0, 1)
+        take(2)
+        q_y(1, 0, 0)
+        q_y(1, 0, 1)
+        q_waves(3, 0, 1)
+        q_waves(3, 1, 1)
+        store_codes(1, 0)
+        lay_y("gpsimd", 2, 0, 0, gated=True)
+        lay_y("gpsimd", 2, 0, 1)
+        take(4)
+        turn_and_store(2, 1, 0)
+        turn_and_store(2, 1, 1)
+        lay_y("scalar", 2, 1, 0)
+        lay_y("scalar", 2, 1, 1)
+        take(2)
+        q_y(1, 1, 0)
+        q_c(3)
+        q_y(1, 1, 1)
+        q_y(2, 0, 0)
+        q_y(2, 0, 1)
+        store_codes(1, 1)
+        store_scales(0)
+        store_codes(2, 0)
+        take(4)
+        turn_and_store(3, 0, 0)
+        turn_and_store(3, 0, 1)
+        q_y(2, 1, 0)
+        q_y(2, 1, 1)
+        store_codes(2, 1)
+        lay_y("gpsimd", 3, 0, 0, gated=True)
+        take(2)
+        turn_and_store(3, 1, 0)
+        take(2)
+        lay_y("vector", 3, 0, 1)
+        q_y(3, 0, 0)
+        lay_y("vector", 3, 1, 0)
+        q_y(3, 0, 1)
+        store_codes(3, 0)
+        turn_and_store(3, 1, 1)
+        lay_y("vector", 3, 1, 1)
+        q_y(3, 1, 0)
+        q_y(3, 1, 1)
+        store_codes(3, 1)
+        store_scales(2)

@@ -22,7 +22,7 @@ K_PASS = 512
 WIDE = 512
 HALF = 256
 CHUNKS = N // WIDE
-SLOTS = 10
+SLOTS = 6
 MX_BANKS = 4
 TR_BANKS = 4
 
@@ -42,12 +42,12 @@ def tile_delay_shrink_channel_k4_kernel(
 
         ident_f = kept("ident_f", [P, P], F32)
         ident_b = kept("ident_b", [P, P], BF16)
-        front_col = kept("front_col", [P, CHUNKS, PACK], BF16)
+        front_col = kept("front_col", [P, 2, PACK], BF16)
         los_col = kept("los_col", [P, CHUNKS, PACK], BF16)
         nsr_rows = kept("nsr_rows", [P, P], BF16)
         one_plus = kept("one_plus", [P, PACK], F32)
         wiener = kept("wiener", [P, PACK], F32)
-        front_all = kept("front_all", [P, N], BF16)
+        front_all = [kept("front_all%d" % i, [P, N // 2], BF16) for i in range(2)]
         agc_all = kept("agc_all", [P, M], BF16)
         spread_raw = [kept("spread_raw%d" % i, [P, 2, R], BF16) for i in range(2)]
         spread_bf = [kept("spread_bf%d" % k, [P, L * PACK], BF16) for k in range(2)]
@@ -59,14 +59,10 @@ def tile_delay_shrink_channel_k4_kernel(
         ds_plane = kept("ds_plane", [P, 2, L], U8)
         x_codes = [kept("x_codes%d" % h, [P, 2, WIDE], U32) for h in range(2)]
         xs_plane = kept("xs_plane", [P, 2, M], U8)
-        waves_raw = {}
-        waves_codes = {}
-        waves_scales = {}
-        for g in range(CHUNKS):
-            for k in range(2):
-                waves_raw[g, k] = kept("waves_raw%d%d" % (g, k), [P, PACK, WIDE], BF16)
-                waves_codes[g, k] = kept("waves_codes%d%d" % (g, k), [P, WIDE], U32)
-                waves_scales[g, k] = kept("waves_scales%d%d" % (g, k), [P, WIDE], U8)
+        first_raw = [kept("first_raw%d" % k, [P, PACK, WIDE], BF16) for k in range(2)]
+        waves_raw = {g: kept("waves_raw%d" % g, [P, 2, PACK, WIDE], BF16) for g in range(1, CHUNKS)}
+        waves_codes = [kept("waves_codes%d" % g, [P, 2 * WIDE], U32) for g in range(CHUNKS)]
+        waves_scales = [kept("waves_scales%d" % g, [P, 2 * WIDE], U8) for g in range(CHUNKS)]
         taps_bf = [kept("taps_bf%d" % h, [P, PACK, WIDE], BF16) for h in range(2)]
         shrunk_codes = [kept("shrunk_codes%d" % h, [P, WIDE], U32) for h in range(2)]
         shrunk_scales = [kept("shrunk_scales%d" % h, [P, WIDE], U8) for h in range(2)]
@@ -89,7 +85,8 @@ def tile_delay_shrink_channel_k4_kernel(
 
         def load_waves(g, k):
             src = waves[K_PASS * k : K_PASS * (k + 1), WIDE * g : WIDE * (g + 1)]
-            nc.sync.dma_start(out=waves_raw[g, k][:], in_=src.rearrange("(p j) n -> p j n", j=PACK))
+            dst = first_raw[k][:] if g == 0 else waves_raw[g][:, k, :, :]
+            nc.sync.dma_start(out=dst, in_=src.rearrange("(p j) n -> p j n", j=PACK))
 
         def load_spread(i):
             src = spread.rearrange("(a p) k -> p a k", p=P)
@@ -113,7 +110,7 @@ def tile_delay_shrink_channel_k4_kernel(
         load_waves(0, 0)
         load_spread(1)
         nc.sync.dma_start(out=d_raw[:].bitcast(I32), in_=d_words.rearrange("g p b -> p g b").bitcast(I32))
-        nc.scalar.dma_start(out=front_col[:], in_=front.rearrange("(g p t) -> p g t", g=CHUNKS, t=PACK))
+        nc.scalar.dma_start(out=front_col[:], in_=front[: N // 2].rearrange("(g p t) -> p g t", g=2, t=PACK))
         for q in range(3):
             load_scale_rows(nc.scalar, ds_raw, d_scales, q)
         for q in range(1, 4):
@@ -128,67 +125,89 @@ def tile_delay_shrink_channel_k4_kernel(
         )
         load_scale_rows(nc.scalar, ds_raw, d_scales, 3)
         load_scale_rows(nc.scalar, xs_plane, x_scales, 0)
-        nc.scalar.dma_start(out=los_col[:], in_=los.rearrange("(g p t) -> p g t", g=CHUNKS, t=PACK))
         load_waves(1, 1)
+        nc.sync.dma_start(out=los_col[:], in_=los.rearrange("(g p t) -> p g t", g=CHUNKS, t=PACK))
         nc.sync.dma_start(out=agc_all[:], in_=agc.partition_broadcast(P))
         for g in range(2, CHUNKS):
             for k in range(2):
                 load_waves(g, k)
+        nc.sync.dma_start(out=front_all[1][:], in_=front[N // 2 :].partition_broadcast(P))
 
         free = ["slot%d" % i for i in range(SLOTS)]
         staged = {}
         made = set()
 
-        def interleave(engine, key, rows, gated=False):
+        def half(x):
+            return slice(HALF * x, HALF * (x + 1))
+
+        def stage(key, gated=False):
             tag = free[-1] if gated else free[0]
             free.remove(tag)
-            tile = work.tile([P, HALF * PACK], BF16, name=tag, tag=tag, align_bytes=64)
-            staged[key] = (tag, tile)
+            staged[key] = (tag, work.tile([P, WIDE * PACK], BF16, name=tag, tag=tag, align_bytes=64))
+
+        def lay(engine, key, rows, x=None):
+            tile = staged[key][1][:]
+            if x is not None:
+                tile = tile[:, PACK * HALF * x : PACK * HALF * (x + 1)]
+            runs = rows.shape[1]
             if engine == "gpsimd":
                 nc.gpsimd.tensor_scalar(
-                    out=tile[:].rearrange("p (m t) -> p m t", t=PACK),
-                    in0=rows.rearrange("p t m -> p m t"),
+                    out=tile.rearrange("p (k m t) -> p k m t", k=runs, t=PACK),
+                    in0=rows.rearrange("p k t m -> p k m t"),
                     scalar1=1.0, scalar2=0.0, op0=ALU.mult, op1=ALU.add,
                 )
             else:
-                dst = tile[:].rearrange("p (c i t) -> p c t i", i=4, t=PACK)
-                src = rows.rearrange("p t (c i) -> p c t i", i=4)
+                dst = tile.rearrange("p (k c i t) -> p k c t i", k=runs, i=4, t=PACK)
+                src = rows.rearrange("p k t (c i) -> p k c t i", i=4)
                 if engine == "vector":
                     nc.vector.tensor_copy(out=dst, in_=src)
                 else:
                     nc.scalar.copy(out=dst, in_=src)
 
-        def quantise(key, codes, scales):
+        def quantise(key, codes, scales, x=None):
             tag, tile = staged[key]
-            nc.vector.quantize_mx(out=codes.bitcast(FP8X4), scales=scales, in_=tile[:])
-            free.append(tag)
-            made.add(key)
+            if x is None:
+                nc.vector.quantize_mx(out=codes.bitcast(FP8X4), scales=scales, in_=tile[:])
+            else:
+                src = tile[:, PACK * HALF * x : PACK * HALF * (x + 1)]
+                nc.vector.quantize_mx(out=codes[:, half(x)].bitcast(FP8X4), scales=scales[:, half(x)], in_=src)
+            if x != 0:
+                free.append(tag)
 
-        def half(x):
-            return slice(HALF * x, HALF * (x + 1))
+        def one_run(rows, x):
+            return (rows if x is None else rows[:, :, half(x)]).unsqueeze(1)
 
-        def lay_waves(engine, g, k, x, gated=False):
-            interleave(engine, ("w", g, k, x), waves_raw[g, k][:, :, half(x)], gated)
+        def lay_waves(engine, g, x, gated=False):
+            stage(("w", g, x), gated)
+            lay(engine, ("w", g, x), waves_raw[g][:, :, :, half(x)])
 
-        def q_waves(g, k, x):
-            quantise(("w", g, k, x), waves_codes[g, k][:, half(x)], waves_scales[g, k][:, half(x)])
+        def q_waves(g, x):
+            cols = slice(WIDE * x, WIDE * (x + 1))
+            quantise(("w", g, x), waves_codes[g][:, cols], waves_scales[g][:, cols])
+            made.add(("w", g, x))
             fill()
 
-        def lay_taps(engine, h, x, gated=False):
-            interleave(engine, ("s", h, x), taps_bf[h][:, :, half(x)], gated)
+        def lay_taps(engine, h, x=None):
+            lay(engine, ("s", h), one_run(taps_bf[h][:], x), x)
 
-        def q_taps(h, x):
-            quantise(("s", h, x), shrunk_codes[h][:, half(x)], shrunk_scales[h][:, half(x)])
+        def q_taps(h):
+            quantise(("s", h), shrunk_codes[h][:], shrunk_scales[h][:])
+            made.add(("s", h))
             fill()
 
         y_t = {}
 
-        def lay_y(engine, g, h, x, gated=False):
-            interleave(engine, ("y", g, h, x), y_t[g, h][:, :, half(x)], gated)
+        def y_part(g, h, x):
+            if (g, h, x) in y_t:
+                return y_t[g, h, x][:]
+            return y_t[g, h][:] if x is None else y_t[g, h][:, :, half(x)]
 
-        def q_y(g, h, x):
-            cols = slice(WIDE * h + HALF * x, WIDE * h + HALF * (x + 1))
-            quantise(("y", g, h, x), y_codes[g, h][:, half(x)], y_scales[4 * g :, cols])
+        def lay_y(engine, g, h, x=None):
+            lay(engine, ("y", g, h), y_part(g, h, x).unsqueeze(1), x)
+
+        def q_y(g, h):
+            quantise(("y", g, h), y_codes[g, h][:], y_scales[4 * g :, WIDE * h : WIDE * (h + 1)])
+            store_codes(g, h)
 
         def store_codes(g, h):
             dst = out_1[g].rearrange("p m t -> p (m t)")[:, 4 * WIDE * h : 4 * WIDE * (h + 1)]
@@ -221,22 +240,24 @@ def tile_delay_shrink_channel_k4_kernel(
             nc.scalar.activation(out=taps_bf[h][:, s, :], in_=acc[:], func=ACT.Copy, scale=wiener[:, s : s + 1])
 
         def mm_c(acc, g, b):
-            cols = slice(P * b, P * (b + 1))
             for s in range(PACK):
                 for k in range(2):
+                    first = (WIDE * k + P * b) if g == 0 else (WIDE * (b // 2) + HALF * k + P * (b % 2))
+                    cols = slice(first, first + P)
                     nc.tensor.matmul_mx(
                         out=acc[:, P * s : P * (s + 1)],
                         lhsT=spread_codes[k][:, P * s : P * (s + 1)].bitcast(FP8X4),
                         lhsT_scale=spread_scales[k][:, P * s : P * (s + 1)],
-                        rhs=waves_codes[g, k][:, cols].bitcast(FP8X4),
-                        rhs_scale=waves_scales[g, k][:, cols],
+                        rhs=waves_codes[g][:, cols].bitcast(FP8X4),
+                        rhs_scale=waves_scales[g][:, cols],
                         start=(k == 0), stop=(k == 1),
                     )
 
         def read_c(acc, g, b):
             a = slice(32 * b, 32 * (b + 1))
             dst = c_bf[g][:].rearrange("p (t a s) -> p t a s", t=PACK, s=PACK)[:, :, a, :]
-            gain = front_all[:, WIDE * g : WIDE * (g + 1)].rearrange("p (t a) -> p t a", t=PACK)[:, :, a]
+            order = "p (t a) -> p t a" if g < 2 else "p (a t) -> p t a"
+            gain = front_all[g // 2][:, WIDE * (g % 2) : WIDE * (g % 2 + 1)].rearrange(order, t=PACK)[:, :, a]
             nc.vector.tensor_tensor(
                 out=dst,
                 in0=acc[:].rearrange("p (s a t) -> p t a s", s=PACK, t=PACK),
@@ -256,7 +277,7 @@ def tile_delay_shrink_channel_k4_kernel(
 
         def read_est(acc, g, h, t):
             if t == 0:
-                tag = "y_t%d" % (count["yt"] % 4)
+                tag = "y_t%d" % (count["yt"] % 3)
                 count["yt"] = count["yt"] + 1
                 y_t[g, h] = work.tile([P, PACK, WIDE], F32, name=tag, tag=tag, align_bytes=64)
             nc.vector.scalar_tensor_tensor(
@@ -277,22 +298,21 @@ def tile_delay_shrink_channel_k4_kernel(
                 )
 
         def read_est_half(acc, g, h, x, pair):
-            if x == 0 and pair == 0:
-                tag = "y_t%d" % (count["yt"] % 4)
-                count["yt"] = count["yt"] + 1
-                y_t[g, h] = work.tile([P, PACK, WIDE], F32, name=tag, tag=tag, align_bytes=64)
+            if pair == 0:
+                tag = "y_half%d%d" % (h, x)
+                y_t[g, h, x] = work.tile([P, PACK, HALF], F32, name=tag, tag=tag, align_bytes=64)
             for e in range(2):
                 t = 2 * pair + e
                 nc.vector.scalar_tensor_tensor(
-                    out=y_t[g, h][:, t, half(x)], in0=acc[:, half(e)], scalar=los_col[:, g, t : t + 1],
+                    out=y_t[g, h, x][:, t, :], in0=acc[:, half(e)], scalar=los_col[:, g, t : t + 1],
                     in1=agc_all[:, WIDE * h + HALF * x : WIDE * h + HALF * (x + 1)], op0=ALU.add, op1=ALU.mult,
                 )
 
         def needs_c(g, b):
-            return [("w", g, k, b // 2) for k in range(2)] + ["spread"]
+            return [("w", g, b // 2), "spread"]
 
         def needs_est(g, h):
-            return [("c", g), ("s", h, 0), ("s", h, 1)]
+            return [("c", g), ("s", h)]
 
         def mm_front(acc, i):
             view = acc[:].bitcast(BF16)
@@ -301,7 +321,7 @@ def tile_delay_shrink_channel_k4_kernel(
                 nc.tensor.transpose(view[:, P * c : P * (c + 1)], col.to_broadcast([P, P]), ident_b[:])
 
         def read_front(acc, i):
-            dst = front_all[:, 1024 * i : 1024 * (i + 1)]
+            dst = front_all[i][:]
             nc.scalar.copy(out=dst, in_=acc[:].bitcast(BF16))
 
         def c_banks(g, banks):
@@ -310,18 +330,16 @@ def tile_delay_shrink_channel_k4_kernel(
         def est_banks(g, h):
             return [(mm_est, read_est, (g, h, t), needs_est(g, h)) for t in range(PACK)]
 
-        line = [(mm_front, read_front, (i,), []) for i in range(2)]
+        line = [(mm_front, read_front, (0,), [])]
         line.extend([(mm_taps, read_taps, (0, s), ["d"]) for s in range(PACK)])
         line.extend(c_banks(0, range(4)))
         for g in range(CHUNKS):
             for h in range(2):
-                if (g, h) == (CHUNKS - 1, 1):
+                if g == CHUNKS - 1:
                     for x in range(2):
                         line.extend([(mm_est_half, read_est_half, (g, h, x, pair), needs_est(g, h)) for pair in range(2)])
                 else:
-                    line.extend(est_banks(g, h))
-                if g + 1 < CHUNKS:
-                    line.extend(c_banks(g + 1, range(2 * h, 2 * h + 2)))
+                    line.extend(est_banks(g, h) + c_banks(g + 1, range(2 * h, 2 * h + 2)))
         held = {}
 
         def fill():
@@ -334,23 +352,23 @@ def tile_delay_shrink_channel_k4_kernel(
                 held[count["filled"]] = acc
                 count["filled"] = count["filled"] + 1
 
-        def take(n):
+        def take(n, refill=True):
             for step in range(n):
                 matmuls, reader, args, needs = line[count["taken"]]
                 reader(held[count["taken"]], *args)
                 count["taken"] = count["taken"] + 1
-                fill()
+                if refill:
+                    fill()
 
         def turn_and_store(g, h, x):
-            tag = "y_out%d" % (count["yo"] % 6)
+            tag = "y_out%d" % (count["yo"] % 4)
             count["yo"] = count["yo"] + 1
             y_out = work.tile([P, 2, WIDE], F32, name=tag, tag=tag, align_bytes=64)
             turned = []
             for j in range(2):
                 tr = bank("tr", [P, PACK, P], F32)
-                cols = slice(HALF * x + P * j, HALF * x + P * (j + 1))
                 for t in range(PACK):
-                    nc.tensor.transpose(tr[:, t, :], y_t[g, h][:, t, cols], ident_f[:])
+                    nc.tensor.transpose(tr[:, t, :], y_part(g, h, x)[:, t, P * j : P * (j + 1)], ident_f[:])
                 turned.append(tr)
             for j in range(2):
                 nc.scalar.copy(
@@ -362,11 +380,10 @@ def tile_delay_shrink_channel_k4_kernel(
             nc.sync.dma_start(out=rows.rearrange("(j p) n -> p j n", p=P), in_=y_out[:])
 
         fill()
-        take(2)
-        lay_waves("vector", 0, 0, 0)
-        lay_waves("vector", 0, 0, 1)
-        q_waves(0, 0, 0)
-        q_waves(0, 0, 1)
+        take(1)
+        stage(("first", 0))
+        lay("vector", ("first", 0), one_run(first_raw[0][:], None))
+        quantise(("first", 0), waves_codes[0][:, :WIDE], waves_scales[0][:, :WIDE])
         for i in range(2):
             for k in range(2):
                 tr = bank("tr", [P, 2, 2, P], F32)
@@ -395,132 +412,89 @@ def tile_delay_shrink_channel_k4_kernel(
         nc.vector.tensor_scalar(out=one_plus[:], in0=tr_nsr[:, 0:PACK], scalar1=1.0, scalar2=None, op0=ALU.add)
         q_spread(0)
         nc.vector.reciprocal(out=wiener[:], in_=one_plus[:])
+        stage(("first", 1))
         q_spread(1)
         made.add("spread")
         take(4)
-        lay_waves("vector", 0, 1, 0)
-        lay_waves("vector", 0, 1, 1)
-        q_waves(0, 1, 0)
-        q_waves(0, 1, 1)
+        lay("vector", ("first", 1), one_run(first_raw[1][:], 0), 0)
+        lay("vector", ("first", 1), one_run(first_raw[1][:], 1), 1)
+        quantise(("first", 1), waves_codes[0][:, WIDE:], waves_scales[0][:, WIDE:], 0)
+        made.add(("w", 0, 0))
+        fill()
+        quantise(("first", 1), waves_codes[0][:, WIDE:], waves_scales[0][:, WIDE:], 1)
+        made.add(("w", 0, 1))
+        fill()
+        stage(("s", 0), gated=True)
+        lay_taps("gpsimd", 0, 0)
         second_taps = []
-
-        def second_taps_bank(s):
+        for s in range(PACK):
             acc = bank("tr", [P, WIDE], F32)
             mm_taps(acc, 1, s)
             second_taps.append(acc)
-
-        lay_taps("gpsimd", 0, 0, gated=True)
-        lay_taps("gpsimd", 0, 1)
-        for s in range(PACK):
-            second_taps_bank(s)
-        lay_waves("scalar", 1, 0, 0)
-        lay_waves("scalar", 1, 1, 0)
+        lay_waves("scalar", 1, 0)
         take(4)
-        q_taps(0, 0)
+        lay_taps("vector", 0, 1)
         q_c(0)
-        q_taps(0, 1)
-        q_waves(1, 0, 0)
-        q_waves(1, 1, 0)
+        q_taps(0)
+        q_waves(1, 0)
         for s in range(PACK):
             read_taps(second_taps[s], 1, s)
-        lay_taps("scalar", 1, 0)
-        lay_taps("scalar", 1, 1)
+        lay_waves("gpsimd", 1, 1, gated=True)
+        stage(("s", 1))
+        lay_taps("scalar", 1)
 
-        lay_waves("gpsimd", 1, 0, 1, gated=True)
-        lay_waves("gpsimd", 1, 1, 1)
-        take(4)
-        turn_and_store(0, 0, 0)
-        turn_and_store(0, 0, 1)
-        lay_y("scalar", 0, 0, 0)
-        lay_y("scalar", 0, 0, 1)
-        take(2)
-        q_waves(1, 0, 1)
-        q_taps(1, 0)
-        q_taps(1, 1)
-        q_waves(1, 1, 1)
-        lay_waves("gpsimd", 2, 0, 0, gated=True)
-        lay_waves("gpsimd", 2, 1, 0)
-        take(4)
-        turn_and_store(0, 1, 0)
-        turn_and_store(0, 1, 1)
-        lay_y("scalar", 0, 1, 0)
-        lay_y("scalar", 0, 1, 1)
-        take(2)
-        q_waves(2, 0, 0)
-        q_c(1)
-        q_y(0, 0, 0)
-        q_y(0, 0, 1)
-        q_waves(2, 1, 0)
-        store_codes(0, 0)
-        lay_waves("gpsimd", 2, 0, 1, gated=True)
-        lay_waves("gpsimd", 2, 1, 1)
-        take(4)
-        turn_and_store(1, 0, 0)
-        turn_and_store(1, 0, 1)
-        lay_y("scalar", 1, 0, 0)
-        lay_y("scalar", 1, 0, 1)
-        take(2)
-        q_waves(2, 0, 1)
-        q_waves(2, 1, 1)
-        lay_waves("gpsimd", 3, 0, 0, gated=True)
-        lay_waves("gpsimd", 3, 1, 0)
-        take(4)
-        turn_and_store(1, 1, 0)
-        turn_and_store(1, 1, 1)
-        lay_y("scalar", 1, 1, 0)
-        lay_y("scalar", 1, 1, 1)
-        take(2)
-        q_waves(3, 0, 0)
-        q_c(2)
-        q_y(0, 1, 0)
-        q_y(0, 1, 1)
-        q_waves(3, 1, 0)
-        store_codes(0, 1)
-        lay_waves("gpsimd", 3, 0, 1, gated=True)
-        lay_waves("gpsimd", 3, 1, 1)
-        take(4)
-        turn_and_store(2, 0, 0)
-        turn_and_store(2, 0, 1)
-        take(2)
-        q_y(1, 0, 0)
-        q_y(1, 0, 1)
-        q_waves(3, 0, 1)
-        q_waves(3, 1, 1)
-        store_codes(1, 0)
-        lay_y("gpsimd", 2, 0, 0, gated=True)
-        lay_y("gpsimd", 2, 0, 1)
-        take(4)
-        turn_and_store(2, 1, 0)
-        turn_and_store(2, 1, 1)
-        lay_y("scalar", 2, 1, 0)
-        lay_y("scalar", 2, 1, 1)
-        take(2)
-        q_y(1, 1, 0)
-        q_c(3)
-        q_y(1, 1, 1)
-        q_y(2, 0, 0)
-        q_y(2, 0, 1)
-        store_codes(1, 1)
-        store_scales(0)
-        store_codes(2, 0)
-        take(4)
+        for g in range(CHUNKS - 1):
+            take(4)
+            turn_and_store(g, 0, 0)
+            turn_and_store(g, 0, 1)
+            if g < 2:
+                stage(("y", g, 0))
+                lay_y("scalar", g, 0)
+            take(2)
+            if g == 0:
+                q_taps(1)
+            else:
+                q_y(g - 1, 1)
+            if g == 2:
+                store_scales(0)
+            q_waves(g + 1, 1)
+            if g < 2:
+                lay_waves("gpsimd", g + 2, 0, gated=True)
+            else:
+                stage(("y", g, 0), gated=True)
+                lay_y("gpsimd", g, 0)
+            take(4)
+            turn_and_store(g, 1, 0)
+            turn_and_store(g, 1, 1)
+            stage(("y", g, 1))
+            lay_y("scalar", g, 1, None if g < 2 else 1)
+            take(2)
+            q_c(g + 1)
+            q_y(g, 0)
+            if g < 2:
+                q_waves(g + 2, 0)
+                lay_waves("gpsimd", g + 2, 1, gated=True)
+        stage(("y", 2, 1, 0), gated=True)
+        lay("gpsimd", ("y", 2, 1, 0), one_run(y_t[2, 1][:], 0), 0)
+        take(2, False)
         turn_and_store(3, 0, 0)
+        fill()
+        stage(("y", 3, 0))
+        lay_y("gpsimd", 3, 0, 0)
+        take(2, False)
         turn_and_store(3, 0, 1)
-        q_y(2, 1, 0)
-        q_y(2, 1, 1)
-        store_codes(2, 1)
-        lay_y("gpsimd", 3, 0, 0, gated=True)
+        fill()
+        lay_y("gpsimd", 3, 0, 1)
         take(2)
         turn_and_store(3, 1, 0)
         take(2)
-        lay_y("vector", 3, 0, 1)
-        q_y(3, 0, 0)
+        stage(("y", 3, 1))
         lay_y("vector", 3, 1, 0)
-        q_y(3, 0, 1)
-        store_codes(3, 0)
+        quantise(("y", 2, 1, 0), y_codes[2, 1][:], y_scales[8:, WIDE:], 0)
+        quantise(("y", 2, 1), y_codes[2, 1][:], y_scales[8:, WIDE:], 1)
+        store_codes(2, 1)
         turn_and_store(3, 1, 1)
         lay_y("vector", 3, 1, 1)
-        q_y(3, 1, 0)
-        q_y(3, 1, 1)
-        store_codes(3, 1)
+        q_y(3, 0)
+        q_y(3, 1)
         store_scales(2)

@@ -18,13 +18,17 @@ ACT = mybir.ActivationFunctionType
 
 P = 128
 PACK = 4
-K_PASS = 512
+K_PASS = P * PACK
 WIDE = 512
-HALF = 256
+PART = WIDE // 2
 CHUNKS = N // WIDE
-SLOTS = 6
-MX_BANKS = 4
-TR_BANKS = 4
+LAST = CHUNKS - 1
+QUADRANTS = 4
+PRODUCT_BANKS = 4
+TURN_BANKS = 4
+STAGING_TILES = 6
+Y_T_TILES = 3
+Y_OUT_TILES = 4
 
 
 def tile_delay_shrink_channel_k4_kernel(
@@ -40,6 +44,15 @@ def tile_delay_shrink_channel_k4_kernel(
         def kept(name, shape, dtype):
             return keep.tile(shape, dtype, name=name, align_bytes=64)
 
+        def part(x):
+            return slice(PART * x, PART * (x + 1))
+
+        def wide(i):
+            return slice(WIDE * i, WIDE * (i + 1))
+
+        def block(i):
+            return slice(P * i, P * (i + 1))
+
         ident_f = kept("ident_f", [P, P], F32)
         ident_b = kept("ident_b", [P, P], BF16)
         front_col = kept("front_col", [P, 2, PACK], BF16)
@@ -48,7 +61,7 @@ def tile_delay_shrink_channel_k4_kernel(
         one_plus = kept("one_plus", [P, PACK], F32)
         wiener = kept("wiener", [P, PACK], F32)
         front_all = [kept("front_all%d" % i, [P, N // 2], BF16) for i in range(2)]
-        agc_all = kept("agc_all", [P, M], BF16)
+        agc_all = [kept("agc_all%d" % h, [P, WIDE], BF16) for h in range(2)]
         spread_raw = [kept("spread_raw%d" % i, [P, 2, R], BF16) for i in range(2)]
         spread_bf = [kept("spread_bf%d" % k, [P, L * PACK], BF16) for k in range(2)]
         spread_codes = [kept("spread_codes%d" % k, [P, L], U32) for k in range(2)]
@@ -69,36 +82,37 @@ def tile_delay_shrink_channel_k4_kernel(
         c_bf = [kept("c_bf%d" % g, [P, WIDE * PACK], BF16) for g in range(CHUNKS)]
         c_codes = [kept("c_codes%d" % g, [P, WIDE], U32) for g in range(CHUNKS)]
         c_scales = [kept("c_scales%d" % g, [P, WIDE], U8) for g in range(CHUNKS)]
-        y_codes = {}
-        for g in range(CHUNKS):
-            for h in range(2):
-                y_codes[g, h] = kept("y_codes%d%d" % (g, h), [P, WIDE], U32)
+        y_codes = {(g, h): kept("y_codes%d%d" % (g, h), [P, WIDE], U32) for g in range(CHUNKS) for h in range(2)}
         y_scales = kept("y_scales", [P, M], U8)
 
-        count = {"mx": 0, "tr": 0, "yt": 0, "yo": 0, "filled": 0, "taken": 0}
+        count = {"product": 0, "turn": 0, "y_t": 0, "y_out": 0, "filled": 0, "taken": 0}
 
-        def bank(kind, shape, dtype):
-            n_banks = MX_BANKS if kind == "mx" else TR_BANKS
-            tag = "%s%d" % (kind, count[kind] % n_banks)
+        def rotating(pool, kind, depth, shape, dtype):
+            tag = "%s%d" % (kind, count[kind] % depth)
             count[kind] = count[kind] + 1
-            return psum.tile(shape, dtype, name=tag, tag=tag)
+            if pool is psum:
+                return psum.tile(shape, dtype, name=tag, tag=tag)
+            return pool.tile(shape, dtype, name=tag, tag=tag, align_bytes=64)
+
+        def turn_bank(shape, dtype):
+            return rotating(psum, "turn", TURN_BANKS, shape, dtype)
 
         def load_waves(g, k):
-            src = waves[K_PASS * k : K_PASS * (k + 1), WIDE * g : WIDE * (g + 1)]
+            src = waves[K_PASS * k : K_PASS * (k + 1), wide(g)]
             dst = first_raw[k][:] if g == 0 else waves_raw[g][:, k, :, :]
-            nc.sync.dma_start(out=dst, in_=src.rearrange("(p j) n -> p j n", j=PACK))
+            nc.sync.dma_start(out=dst, in_=src.rearrange("(p t) n -> p t n", t=PACK))
 
         def load_spread(i):
             src = spread.rearrange("(a p) k -> p a k", p=P)
             nc.sync.dma_start(out=spread_raw[i][:], in_=src[:, 2 * i : 2 * i + 2, :])
 
         def load_x(h):
-            src = x_words.rearrange("g p m t -> p g (m t)")[:, :, 4 * WIDE * h : 4 * WIDE * (h + 1)]
+            src = x_words.rearrange("k p m t -> p k (m t)")[:, :, PACK * WIDE * h : PACK * WIDE * (h + 1)]
             nc.sync.dma_start(out=x_codes[h][:].bitcast(I32), in_=src.bitcast(I32))
 
-        def load_scale_rows(queue, plane, rows, q):
-            src = rows[:, 4 * q : 4 * q + 4, :].rearrange("g r n -> r g n")
-            queue.dma_start(out=plane[32 * q : 32 * q + 4, :, :].bitcast(I32), in_=src.bitcast(I32))
+        def load_scale_rows(queue, plane, rows, quadrant):
+            src = rows[:, 4 * quadrant : 4 * quadrant + 4, :].rearrange("k r n -> r k n")
+            queue.dma_start(out=plane[32 * quadrant : 32 * quadrant + 4, :, :].bitcast(I32), in_=src.bitcast(I32))
 
         make_identity(nc, ident_f[:])
         nc.vector.memset(ds_raw[:].bitcast(I32), 0)
@@ -109,12 +123,12 @@ def tile_delay_shrink_channel_k4_kernel(
         load_spread(0)
         load_waves(0, 0)
         load_spread(1)
-        nc.sync.dma_start(out=d_raw[:].bitcast(I32), in_=d_words.rearrange("g p b -> p g b").bitcast(I32))
+        nc.sync.dma_start(out=d_raw[:].bitcast(I32), in_=d_words.rearrange("k p b -> p k b").bitcast(I32))
         nc.scalar.dma_start(out=front_col[:], in_=front[: N // 2].rearrange("(g p t) -> p g t", g=2, t=PACK))
-        for q in range(3):
-            load_scale_rows(nc.scalar, ds_raw, d_scales, q)
-        for q in range(1, 4):
-            load_scale_rows(nc.gpsimd, xs_plane, x_scales, q)
+        for quadrant in range(QUADRANTS - 1):
+            load_scale_rows(nc.scalar, ds_raw, d_scales, quadrant)
+        for quadrant in range(1, QUADRANTS):
+            load_scale_rows(nc.gpsimd, xs_plane, x_scales, quadrant)
         load_x(0)
         load_waves(0, 1)
         load_x(1)
@@ -123,34 +137,34 @@ def tile_delay_shrink_channel_k4_kernel(
             out=nsr_rows[0:PACK, :].rearrange("s (q r) -> s q r", r=8),
             in_=nsr.rearrange("(q s r) -> s q r", s=PACK, r=8),
         )
-        load_scale_rows(nc.scalar, ds_raw, d_scales, 3)
+        load_scale_rows(nc.scalar, ds_raw, d_scales, QUADRANTS - 1)
         load_scale_rows(nc.scalar, xs_plane, x_scales, 0)
         load_waves(1, 1)
+        nc.sync.dma_start(out=agc_all[0][:], in_=agc[wide(0)].partition_broadcast(P))
         nc.sync.dma_start(out=los_col[:], in_=los.rearrange("(g p t) -> p g t", g=CHUNKS, t=PACK))
-        nc.sync.dma_start(out=agc_all[:], in_=agc.partition_broadcast(P))
+        nc.sync.dma_start(out=agc_all[1][:], in_=agc[wide(1)].partition_broadcast(P))
         for g in range(2, CHUNKS):
             for k in range(2):
                 load_waves(g, k)
         nc.sync.dma_start(out=front_all[1][:], in_=front[N // 2 :].partition_broadcast(P))
 
-        free = ["slot%d" % i for i in range(SLOTS)]
+        free = ["staging%d" % i for i in range(STAGING_TILES)]
         staged = {}
         made = set()
 
-        def half(x):
-            return slice(HALF * x, HALF * (x + 1))
-
-        def stage(key, gated=False):
-            tag = free[-1] if gated else free[0]
+        def stage(key, after_last_quantise=False):
+            tag = free[-1] if after_last_quantise else free[0]
             free.remove(tag)
             staged[key] = (tag, work.tile([P, WIDE * PACK], BF16, name=tag, tag=tag, align_bytes=64))
 
-        def lay(engine, key, rows, x=None):
+        def staged_part(key, x):
             tile = staged[key][1][:]
-            if x is not None:
-                tile = tile[:, PACK * HALF * x : PACK * HALF * (x + 1)]
+            return tile if x is None else tile[:, PACK * PART * x : PACK * PART * (x + 1)]
+
+        def interleave(engine, key, rows, x=None):
+            tile = staged_part(key, x)
             runs = rows.shape[1]
-            if engine == "gpsimd":
+            if engine is nc.gpsimd:
                 nc.gpsimd.tensor_scalar(
                     out=tile.rearrange("p (k m t) -> p k m t", k=runs, t=PACK),
                     in0=rows.rearrange("p k t m -> p k m t"),
@@ -159,234 +173,219 @@ def tile_delay_shrink_channel_k4_kernel(
             else:
                 dst = tile.rearrange("p (k c i t) -> p k c t i", k=runs, i=4, t=PACK)
                 src = rows.rearrange("p k t (c i) -> p k c t i", i=4)
-                if engine == "vector":
+                if engine is nc.vector:
                     nc.vector.tensor_copy(out=dst, in_=src)
                 else:
                     nc.scalar.copy(out=dst, in_=src)
 
         def quantise(key, codes, scales, x=None):
-            tag, tile = staged[key]
-            if x is None:
-                nc.vector.quantize_mx(out=codes.bitcast(FP8X4), scales=scales, in_=tile[:])
-            else:
-                src = tile[:, PACK * HALF * x : PACK * HALF * (x + 1)]
-                nc.vector.quantize_mx(out=codes[:, half(x)].bitcast(FP8X4), scales=scales[:, half(x)], in_=src)
+            if x is not None:
+                codes, scales = codes[:, part(x)], scales[:, part(x)]
+            nc.vector.quantize_mx(out=codes.bitcast(FP8X4), scales=scales, in_=staged_part(key, x))
             if x != 0:
-                free.append(tag)
+                free.append(staged[key][0])
 
-        def one_run(rows, x):
-            return (rows if x is None else rows[:, :, half(x)]).unsqueeze(1)
-
-        def lay_waves(engine, g, x, gated=False):
-            stage(("w", g, x), gated)
-            lay(engine, ("w", g, x), waves_raw[g][:, :, :, half(x)])
-
-        def q_waves(g, x):
-            cols = slice(WIDE * x, WIDE * (x + 1))
-            quantise(("w", g, x), waves_codes[g][:, cols], waves_scales[g][:, cols])
-            made.add(("w", g, x))
+        def ready(operand):
+            made.add(operand)
             fill()
 
-        def lay_taps(engine, h, x=None):
-            lay(engine, ("s", h), one_run(taps_bf[h][:], x), x)
+        def one_run(rows, x=None):
+            return (rows if x is None else rows[:, :, part(x)]).unsqueeze(1)
 
-        def q_taps(h):
-            quantise(("s", h), shrunk_codes[h][:], shrunk_scales[h][:])
-            made.add(("s", h))
-            fill()
+        def interleave_waves(engine, g, x, after_last_quantise=False):
+            stage(("waves", g, x), after_last_quantise)
+            interleave(engine, ("waves", g, x), waves_raw[g][:, :, :, part(x)])
+
+        def quantise_waves(g, x):
+            quantise(("waves", g, x), waves_codes[g][:, wide(x)], waves_scales[g][:, wide(x)])
+            ready(("waves", g, x))
+
+        def quantise_first(k, x=None):
+            quantise(("first", k), waves_codes[0][:, wide(k)], waves_scales[0][:, wide(k)], x)
+
+        def quantise_spread(k):
+            nc.vector.quantize_mx(out=spread_codes[k][:].bitcast(FP8X4), scales=spread_scales[k][:], in_=spread_bf[k][:])
+
+        def interleave_shrunk(engine, h, x=None):
+            interleave(engine, ("shrunk", h), one_run(taps_bf[h][:], x), x)
+
+        def quantise_shrunk(h):
+            quantise(("shrunk", h), shrunk_codes[h][:], shrunk_scales[h][:])
+            ready(("shrunk", h))
+
+        def quantise_c(g):
+            nc.vector.quantize_mx(out=c_codes[g][:].bitcast(FP8X4), scales=c_scales[g][:], in_=c_bf[g][:])
+            ready(("c", g))
 
         y_t = {}
 
-        def y_part(g, h, x):
-            if (g, h, x) in y_t:
+        def y_t_part(g, h, x):
+            if g == LAST:
                 return y_t[g, h, x][:]
-            return y_t[g, h][:] if x is None else y_t[g, h][:, :, half(x)]
+            return y_t[g, h][:] if x is None else y_t[g, h][:, :, part(x)]
 
-        def lay_y(engine, g, h, x=None):
-            lay(engine, ("y", g, h), y_part(g, h, x).unsqueeze(1), x)
-
-        def q_y(g, h):
-            quantise(("y", g, h), y_codes[g, h][:], y_scales[4 * g :, WIDE * h : WIDE * (h + 1)])
-            store_codes(g, h)
+        def interleave_y(engine, g, h, x=None):
+            interleave(engine, ("y", g, h), y_t_part(g, h, x).unsqueeze(1), x)
 
         def store_codes(g, h):
-            dst = out_1[g].rearrange("p m t -> p (m t)")[:, 4 * WIDE * h : 4 * WIDE * (h + 1)]
+            dst = out_1[g].rearrange("p m t -> p (m t)")[:, PACK * WIDE * h : PACK * WIDE * (h + 1)]
             nc.sync.dma_start(out=dst.bitcast(I32), in_=y_codes[g, h][:].bitcast(I32))
 
-        def store_scales(g0):
-            for q in range(4):
+        def quantise_y(g, h):
+            quantise(("y", g, h), y_codes[g, h][:], y_scales[4 * g :, wide(h)])
+            store_codes(g, h)
+
+        def store_scales(g):
+            for quadrant in range(QUADRANTS):
+                first = 32 * quadrant + 4 * g
                 nc.sync.dma_start(
-                    out=out_2[g0 : g0 + 2, 4 * q : 4 * q + 4, :].bitcast(I32),
-                    in_=y_scales[32 * q + 4 * g0 : 32 * q + 4 * g0 + 8, :].bitcast(I32),
+                    out=out_2[g : g + 2, 4 * quadrant : 4 * quadrant + 4, :].bitcast(I32),
+                    in_=y_scales[first : first + 8, :].bitcast(I32),
                 )
 
-        def q_c(g):
-            nc.vector.quantize_mx(out=c_codes[g][:].bitcast(FP8X4), scales=c_scales[g][:], in_=c_bf[g][:])
-            made.add(("c", g))
-            fill()
+        def spread_front(acc):
+            for g in range(2):
+                for t in range(PACK):
+                    column = front_col[:, g, t : t + 1].to_broadcast([P, P])
+                    nc.tensor.transpose(acc[:].bitcast(BF16)[:, block(PACK * g + t)], column, ident_b[:])
 
-        def mm_taps(acc, h, s):
+        def read_front(acc):
+            nc.scalar.copy(
+                out=front_all[0][:].rearrange("p (g a t) -> p g a t", g=2, t=PACK),
+                in_=acc[:].bitcast(BF16).rearrange("p (g t a) -> p g a t", g=2, t=PACK),
+            )
+
+        def product_taps(acc, h, s):
             for k in range(2):
                 nc.tensor.matmul_mx(
                     out=acc[:],
                     lhsT=d_codes[:, k, 2 * P * s : 2 * P * (s + 1)].bitcast(FP4X4),
-                    lhsT_scale=ds_plane[:, k, P * s : P * (s + 1)],
+                    lhsT_scale=ds_plane[:, k, block(s)],
                     rhs=x_codes[h][:, k, :].bitcast(FP8X4),
-                    rhs_scale=xs_plane[:, k, WIDE * h : WIDE * (h + 1)],
+                    rhs_scale=xs_plane[:, k, wide(h)],
                     start=(k == 0), stop=(k == 1),
                 )
 
         def read_taps(acc, h, s):
             nc.scalar.activation(out=taps_bf[h][:, s, :], in_=acc[:], func=ACT.Copy, scale=wiener[:, s : s + 1])
 
-        def mm_c(acc, g, b):
+        def product_c(acc, g, b):
             for s in range(PACK):
                 for k in range(2):
-                    first = (WIDE * k + P * b) if g == 0 else (WIDE * (b // 2) + HALF * k + P * (b % 2))
-                    cols = slice(first, first + P)
+                    first = (WIDE * k + P * b) if g == 0 else (WIDE * (b // 2) + PART * k + P * (b % 2))
                     nc.tensor.matmul_mx(
-                        out=acc[:, P * s : P * (s + 1)],
-                        lhsT=spread_codes[k][:, P * s : P * (s + 1)].bitcast(FP8X4),
-                        lhsT_scale=spread_scales[k][:, P * s : P * (s + 1)],
-                        rhs=waves_codes[g][:, cols].bitcast(FP8X4),
-                        rhs_scale=waves_scales[g][:, cols],
+                        out=acc[:, block(s)],
+                        lhsT=spread_codes[k][:, block(s)].bitcast(FP8X4),
+                        lhsT_scale=spread_scales[k][:, block(s)],
+                        rhs=waves_codes[g][:, first : first + P].bitcast(FP8X4),
+                        rhs_scale=waves_scales[g][:, first : first + P],
                         start=(k == 0), stop=(k == 1),
                     )
 
         def read_c(acc, g, b):
-            a = slice(32 * b, 32 * (b + 1))
-            dst = c_bf[g][:].rearrange("p (t a s) -> p t a s", t=PACK, s=PACK)[:, :, a, :]
-            order = "p (t a) -> p t a" if g < 2 else "p (a t) -> p t a"
-            gain = front_all[g // 2][:, WIDE * (g % 2) : WIDE * (g % 2 + 1)].rearrange(order, t=PACK)[:, :, a]
+            own = slice(32 * b, 32 * (b + 1))
+            gain = front_all[g // 2][:, wide(g % 2)].rearrange("p (a t) -> p a t", t=PACK)[:, own, :]
             nc.vector.tensor_tensor(
-                out=dst,
-                in0=acc[:].rearrange("p (s a t) -> p t a s", s=PACK, t=PACK),
-                in1=gain.unsqueeze(3).to_broadcast([P, PACK, 32, PACK]),
+                out=c_bf[g][:].rearrange("p (t a s) -> p a s t", t=PACK, s=PACK)[:, own, :, :],
+                in0=acc[:].rearrange("p (s a t) -> p a s t", s=PACK, t=PACK),
+                in1=gain.unsqueeze(2).to_broadcast([P, 32, PACK, PACK]),
                 op=ALU.mult,
             )
 
-        def mm_est(acc, g, h, t):
+        def multiply_est(acc, g, h, t, cols):
             nc.tensor.matmul_mx(
-                out=acc[:],
-                lhsT=c_codes[g][:, P * t : P * (t + 1)].bitcast(FP8X4),
-                lhsT_scale=c_scales[g][:, P * t : P * (t + 1)],
-                rhs=shrunk_codes[h][:].bitcast(FP8X4),
-                rhs_scale=shrunk_scales[h][:],
+                out=acc,
+                lhsT=c_codes[g][:, block(t)].bitcast(FP8X4),
+                lhsT_scale=c_scales[g][:, block(t)],
+                rhs=shrunk_codes[h][:, cols].bitcast(FP8X4),
+                rhs_scale=shrunk_scales[h][:, cols],
                 start=True, stop=True,
             )
 
-        def read_est(acc, g, h, t):
-            if t == 0:
-                tag = "y_t%d" % (count["yt"] % 3)
-                count["yt"] = count["yt"] + 1
-                y_t[g, h] = work.tile([P, PACK, WIDE], F32, name=tag, tag=tag, align_bytes=64)
+        def finish_y(dst, acc, g, h, t, cols):
             nc.vector.scalar_tensor_tensor(
-                out=y_t[g, h][:, t, :], in0=acc[:], scalar=los_col[:, g, t : t + 1],
-                in1=agc_all[:, WIDE * h : WIDE * (h + 1)], op0=ALU.add, op1=ALU.mult,
+                out=dst, in0=acc, scalar=los_col[:, g, t : t + 1], in1=agc_all[h][:, cols], op0=ALU.add, op1=ALU.mult
             )
 
-        def mm_est_half(acc, g, h, x, pair):
-            for e in range(2):
-                t = 2 * pair + e
-                nc.tensor.matmul_mx(
-                    out=acc[:, half(e)],
-                    lhsT=c_codes[g][:, P * t : P * (t + 1)].bitcast(FP8X4),
-                    lhsT_scale=c_scales[g][:, P * t : P * (t + 1)],
-                    rhs=shrunk_codes[h][:, half(x)].bitcast(FP8X4),
-                    rhs_scale=shrunk_scales[h][:, half(x)],
-                    start=True, stop=True,
-                )
+        def product_est(acc, g, h, t):
+            multiply_est(acc[:], g, h, t, wide(0))
 
-        def read_est_half(acc, g, h, x, pair):
+        def read_est(acc, g, h, t):
+            if t == 0:
+                y_t[g, h] = rotating(work, "y_t", Y_T_TILES, [P, PACK, WIDE], F32)
+            finish_y(y_t[g, h][:, t, :], acc[:], g, h, t, wide(0))
+
+        def product_est_part(acc, h, x, pair):
+            for e in range(2):
+                multiply_est(acc[:, part(e)], LAST, h, 2 * pair + e, part(x))
+
+        def read_est_part(acc, h, x, pair):
             if pair == 0:
-                tag = "y_half%d%d" % (h, x)
-                y_t[g, h, x] = work.tile([P, PACK, HALF], F32, name=tag, tag=tag, align_bytes=64)
+                tag = "y_t_last%d%d" % (h, x)
+                y_t[LAST, h, x] = work.tile([P, PACK, PART], F32, name=tag, tag=tag, align_bytes=64)
             for e in range(2):
                 t = 2 * pair + e
-                nc.vector.scalar_tensor_tensor(
-                    out=y_t[g, h, x][:, t, :], in0=acc[:, half(e)], scalar=los_col[:, g, t : t + 1],
-                    in1=agc_all[:, WIDE * h + HALF * x : WIDE * h + HALF * (x + 1)], op0=ALU.add, op1=ALU.mult,
-                )
-
-        def needs_c(g, b):
-            return [("w", g, b // 2), "spread"]
-
-        def needs_est(g, h):
-            return [("c", g), ("s", h)]
-
-        def mm_front(acc, i):
-            view = acc[:].bitcast(BF16)
-            for c in range(8):
-                col = front_col[:, 2 * i + c // PACK, c % PACK : c % PACK + 1]
-                nc.tensor.transpose(view[:, P * c : P * (c + 1)], col.to_broadcast([P, P]), ident_b[:])
-
-        def read_front(acc, i):
-            dst = front_all[i][:]
-            nc.scalar.copy(out=dst, in_=acc[:].bitcast(BF16))
+                finish_y(y_t[LAST, h, x][:, t, :], acc[:, part(e)], LAST, h, t, part(x))
 
         def c_banks(g, banks):
-            return [(mm_c, read_c, (g, b), needs_c(g, b)) for b in banks]
+            return [(product_c, read_c, (g, b), [("waves", g, b // 2), "spread"]) for b in banks]
 
-        def est_banks(g, h):
-            return [(mm_est, read_est, (g, h, t), needs_est(g, h)) for t in range(PACK)]
-
-        line = [(mm_front, read_front, (0,), [])]
-        line.extend([(mm_taps, read_taps, (0, s), ["d"]) for s in range(PACK)])
+        line = [(spread_front, read_front, (), [])]
+        line.extend([(product_taps, read_taps, (0, s), ["d"]) for s in range(PACK)])
         line.extend(c_banks(0, range(4)))
-        for g in range(CHUNKS):
+        for g in range(LAST):
             for h in range(2):
-                if g == CHUNKS - 1:
-                    for x in range(2):
-                        line.extend([(mm_est_half, read_est_half, (g, h, x, pair), needs_est(g, h)) for pair in range(2)])
-                else:
-                    line.extend(est_banks(g, h) + c_banks(g + 1, range(2 * h, 2 * h + 2)))
-        held = {}
+                line.extend([(product_est, read_est, (g, h, t), [("c", g), ("shrunk", h)]) for t in range(PACK)])
+                line.extend(c_banks(g + 1, range(2 * h, 2 * h + 2)))
+        for h in range(2):
+            for x in range(2):
+                line.extend([(product_est_part, read_est_part, (h, x, pair), [("c", LAST)]) for pair in range(2)])
+        banks = {}
 
         def fill():
-            while count["filled"] < min(len(line), count["taken"] + MX_BANKS):
-                matmuls, reader, args, needs = line[count["filled"]]
-                if not all(n in made for n in needs):
+            while count["filled"] < min(len(line), count["taken"] + PRODUCT_BANKS):
+                product, reader, args, needs = line[count["filled"]]
+                if not all(operand in made for operand in needs):
                     return
-                acc = bank("mx", [P, WIDE], F32)
-                matmuls(acc, *args)
-                held[count["filled"]] = acc
+                acc = rotating(psum, "product", PRODUCT_BANKS, [P, WIDE], F32)
+                product(acc, *args)
+                banks[count["filled"]] = acc
                 count["filled"] = count["filled"] + 1
 
         def take(n, refill=True):
             for step in range(n):
-                matmuls, reader, args, needs = line[count["taken"]]
-                reader(held[count["taken"]], *args)
+                product, reader, args, needs = line[count["taken"]]
+                reader(banks[count["taken"]], *args)
                 count["taken"] = count["taken"] + 1
                 if refill:
                     fill()
 
         def turn_and_store(g, h, x):
-            tag = "y_out%d" % (count["yo"] % 4)
-            count["yo"] = count["yo"] + 1
-            y_out = work.tile([P, 2, WIDE], F32, name=tag, tag=tag, align_bytes=64)
+            y_out = rotating(work, "y_out", Y_OUT_TILES, [P, 2, WIDE], F32)
             turned = []
             for j in range(2):
-                tr = bank("tr", [P, PACK, P], F32)
+                tr = turn_bank([P, PACK, P], F32)
                 for t in range(PACK):
-                    nc.tensor.transpose(tr[:, t, :], y_part(g, h, x)[:, t, P * j : P * (j + 1)], ident_f[:])
+                    nc.tensor.transpose(tr[:, t, :], y_t_part(g, h, x)[:, t, block(j)], ident_f[:])
                 turned.append(tr)
             for j in range(2):
                 nc.scalar.copy(
                     out=y_out[:, j, :].rearrange("p (a t) -> p a t", t=PACK),
                     in_=turned[j][:].rearrange("p t a -> p a t"),
                 )
-            first = WIDE * h + HALF * x
-            rows = out_0[first : first + HALF, WIDE * g : WIDE * (g + 1)]
+            first = WIDE * h + PART * x
+            rows = out_0[first : first + PART, wide(g)]
             nc.sync.dma_start(out=rows.rearrange("(j p) n -> p j n", p=P), in_=y_out[:])
 
         fill()
         take(1)
         stage(("first", 0))
-        lay("vector", ("first", 0), one_run(first_raw[0][:], None))
-        quantise(("first", 0), waves_codes[0][:, :WIDE], waves_scales[0][:, :WIDE])
+        interleave(nc.vector, ("first", 0), one_run(first_raw[0][:]))
+        quantise_first(0)
+
         for i in range(2):
             for k in range(2):
-                tr = bank("tr", [P, 2, 2, P], F32)
+                tr = turn_bank([P, 2, 2, P], F32)
                 for u in range(2):
                     for a in range(2):
                         words = spread_raw[i][:, a, :].bitcast(F32)
@@ -398,103 +397,97 @@ def tile_delay_shrink_channel_k4_kernel(
                 )
         for raw, laid in ((ds_raw, ds_plane), (d_raw, d_codes)):
             nc.vector.tensor_copy(
-                out=laid[:].bitcast(I32).rearrange("p g (s q r) -> p g s q r", s=PACK, q=16),
-                in_=raw[:].bitcast(I32).rearrange("p g (q s r) -> p g s q r", s=PACK, q=16),
+                out=laid[:].bitcast(I32).rearrange("p k (s q r) -> p k s q r", s=PACK, q=16),
+                in_=raw[:].bitcast(I32).rearrange("p k (q s r) -> p k s q r", s=PACK, q=16),
             )
-        tr_nsr = bank("tr", [P, P], BF16)
-        nc.tensor.transpose(tr_nsr[:], nsr_rows[:], ident_b[:])
-        made.add("d")
-        fill()
-
-        def q_spread(k):
-            nc.vector.quantize_mx(out=spread_codes[k][:].bitcast(FP8X4), scales=spread_scales[k][:], in_=spread_bf[k][:])
-
-        nc.vector.tensor_scalar(out=one_plus[:], in0=tr_nsr[:, 0:PACK], scalar1=1.0, scalar2=None, op0=ALU.add)
-        q_spread(0)
+        nsr_turned = turn_bank([P, P], BF16)
+        nc.tensor.transpose(nsr_turned[:], nsr_rows[:], ident_b[:])
+        ready("d")
+        nc.vector.tensor_scalar(out=one_plus[:], in0=nsr_turned[:, 0:PACK], scalar1=1.0, scalar2=None, op0=ALU.add)
+        quantise_spread(0)
         nc.vector.reciprocal(out=wiener[:], in_=one_plus[:])
-        stage(("first", 1))
-        q_spread(1)
+        quantise_spread(1)
         made.add("spread")
-        take(4)
-        lay("vector", ("first", 1), one_run(first_raw[1][:], 0), 0)
-        lay("vector", ("first", 1), one_run(first_raw[1][:], 1), 1)
-        quantise(("first", 1), waves_codes[0][:, WIDE:], waves_scales[0][:, WIDE:], 0)
-        made.add(("w", 0, 0))
-        fill()
-        quantise(("first", 1), waves_codes[0][:, WIDE:], waves_scales[0][:, WIDE:], 1)
-        made.add(("w", 0, 1))
-        fill()
-        stage(("s", 0), gated=True)
-        lay_taps("gpsimd", 0, 0)
+        take(PACK)
+
+        stage(("first", 1))
+        for x in range(2):
+            interleave(nc.vector, ("first", 1), one_run(first_raw[1][:], x), x)
+        for x in range(2):
+            quantise_first(1, x)
+            ready(("waves", 0, x))
+        stage(("shrunk", 0), after_last_quantise=True)
+        interleave_shrunk(nc.gpsimd, 0, 0)
         second_taps = []
         for s in range(PACK):
-            acc = bank("tr", [P, WIDE], F32)
-            mm_taps(acc, 1, s)
+            acc = turn_bank([P, WIDE], F32)
+            product_taps(acc, 1, s)
             second_taps.append(acc)
-        lay_waves("scalar", 1, 0)
+        interleave_waves(nc.scalar, 1, 0)
         take(4)
-        lay_taps("vector", 0, 1)
-        q_c(0)
-        q_taps(0)
-        q_waves(1, 0)
+        interleave_shrunk(nc.vector, 0, 1)
+        quantise_c(0)
+        quantise_shrunk(0)
+        quantise_waves(1, 0)
         for s in range(PACK):
             read_taps(second_taps[s], 1, s)
-        lay_waves("gpsimd", 1, 1, gated=True)
-        stage(("s", 1))
-        lay_taps("scalar", 1)
+        interleave_waves(nc.gpsimd, 1, 1, after_last_quantise=True)
+        stage(("shrunk", 1))
+        interleave_shrunk(nc.scalar, 1)
 
-        for g in range(CHUNKS - 1):
-            take(4)
+        for g in range(LAST):
+            waves_left = g + 2 < CHUNKS
+            take(PACK)
             turn_and_store(g, 0, 0)
             turn_and_store(g, 0, 1)
-            if g < 2:
+            if waves_left:
                 stage(("y", g, 0))
-                lay_y("scalar", g, 0)
+                interleave_y(nc.scalar, g, 0)
             take(2)
             if g == 0:
-                q_taps(1)
+                quantise_shrunk(1)
             else:
-                q_y(g - 1, 1)
-            if g == 2:
+                quantise_y(g - 1, 1)
+            if not waves_left:
                 store_scales(0)
-            q_waves(g + 1, 1)
-            if g < 2:
-                lay_waves("gpsimd", g + 2, 0, gated=True)
+            quantise_waves(g + 1, 1)
+
+            if waves_left:
+                interleave_waves(nc.gpsimd, g + 2, 0, after_last_quantise=True)
             else:
-                stage(("y", g, 0), gated=True)
-                lay_y("gpsimd", g, 0)
-            take(4)
+                stage(("y", g, 0), after_last_quantise=True)
+                interleave_y(nc.gpsimd, g, 0)
+            take(PACK)
             turn_and_store(g, 1, 0)
             turn_and_store(g, 1, 1)
             stage(("y", g, 1))
-            lay_y("scalar", g, 1, None if g < 2 else 1)
+            interleave_y(nc.scalar, g, 1, None if waves_left else 1)
             take(2)
-            q_c(g + 1)
-            q_y(g, 0)
-            if g < 2:
-                q_waves(g + 2, 0)
-                lay_waves("gpsimd", g + 2, 1, gated=True)
-        stage(("y", 2, 1, 0), gated=True)
-        lay("gpsimd", ("y", 2, 1, 0), one_run(y_t[2, 1][:], 0), 0)
-        take(2, False)
-        turn_and_store(3, 0, 0)
-        fill()
-        stage(("y", 3, 0))
-        lay_y("gpsimd", 3, 0, 0)
-        take(2, False)
-        turn_and_store(3, 0, 1)
-        fill()
-        lay_y("gpsimd", 3, 0, 1)
+            quantise_c(g + 1)
+            quantise_y(g, 0)
+            if waves_left:
+                quantise_waves(g + 2, 0)
+                interleave_waves(nc.gpsimd, g + 2, 1, after_last_quantise=True)
+
+        before = LAST - 1
+        stage(("y", before, 1, 0), after_last_quantise=True)
+        interleave(nc.gpsimd, ("y", before, 1, 0), one_run(y_t[before, 1][:], 0), 0)
+        stage(("y", LAST, 0))
+        for x in range(2):
+            take(2, refill=False)
+            turn_and_store(LAST, 0, x)
+            fill()
+            interleave_y(nc.gpsimd, LAST, 0, x)
         take(2)
-        turn_and_store(3, 1, 0)
+        turn_and_store(LAST, 1, 0)
         take(2)
-        stage(("y", 3, 1))
-        lay_y("vector", 3, 1, 0)
-        quantise(("y", 2, 1, 0), y_codes[2, 1][:], y_scales[8:, WIDE:], 0)
-        quantise(("y", 2, 1), y_codes[2, 1][:], y_scales[8:, WIDE:], 1)
-        store_codes(2, 1)
-        turn_and_store(3, 1, 1)
-        lay_y("vector", 3, 1, 1)
-        q_y(3, 0)
-        q_y(3, 1)
-        store_scales(2)
+        stage(("y", LAST, 1))
+        interleave_y(nc.vector, LAST, 1, 0)
+        quantise(("y", before, 1, 0), y_codes[before, 1][:], y_scales[4 * before :, wide(1)], 0)
+        quantise(("y", before, 1), y_codes[before, 1][:], y_scales[4 * before :, wide(1)], 1)
+        store_codes(before, 1)
+        turn_and_store(LAST, 1, 1)
+        interleave_y(nc.vector, LAST, 1, 1)
+        quantise_y(LAST, 0)
+        quantise_y(LAST, 1)
+        store_scales(before)

from contextlib import ExitStack

import concourse.mybir as mybir
from concourse.masks import make_identity

M, PILOTS, L, R, N = 1024, 1024, 512, 1024, 2048
FLOPS = 2 * (M * PILOTS * L + L * R * N + M * L * N)

F32 = mybir.dt.float32
BF16 = mybir.dt.bfloat16
I32 = mybir.dt.int32
U32 = mybir.dt.uint32
U8 = mybir.dt.uint8
FP8X4 = mybir.dt.float8_e4m3fn_x4
FP4X4 = mybir.dt.float4_e2m1fn_x4
ALU = mybir.AluOpType
ACT = mybir.ActivationFunctionType

P = 128
PACK = 4
K_PASS = P * PACK
WIDE = 512
PART = WIDE // 2
CHUNKS = N // WIDE
LAST = CHUNKS - 1
QUADRANTS = 4
PRODUCT_BANKS = 4
TURN_BANKS = 4
STAGING_TILES = 6
Y_T_TILES = 3
Y_OUT_TILES = 4


def tile_delay_shrink_channel_k4_kernel(
    tc, x_words, x_scales, d_words, d_scales, spread, waves, nsr, front, los, agc, out_0, out_1, out_2
):
    nc = tc.nc
    with ExitStack() as ctx:
        keep = ctx.enter_context(tc.tile_pool(name="keep", bufs=1))
        work = ctx.enter_context(tc.tile_pool(name="work", bufs=1))
        psum = ctx.enter_context(tc.psum_pool(name="psum", bufs=1))
        ctx.enter_context(tc.manual_schedule())

        def kept(name, shape, dtype):
            return keep.tile(shape, dtype, name=name, align_bytes=64)

        def part(x):
            return slice(PART * x, PART * (x + 1))

        def wide(i):
            return slice(WIDE * i, WIDE * (i + 1))

        def block(i):
            return slice(P * i, P * (i + 1))

        ident_f = kept("ident_f", [P, P], F32)
        ident_b = kept("ident_b", [P, P], BF16)
        front_col = kept("front_col", [P, 2, PACK], BF16)
        los_col = kept("los_col", [P, CHUNKS, PACK], BF16)
        nsr_rows = kept("nsr_rows", [P, P], BF16)
        one_plus = kept("one_plus", [P, PACK], F32)
        wiener = kept("wiener", [P, PACK], F32)
        front_all = [kept("front_all%d" % i, [P, N // 2], BF16) for i in range(2)]
        agc_all = [kept("agc_all%d" % h, [P, WIDE], BF16) for h in range(2)]
        spread_raw = [kept("spread_raw%d" % i, [P, 2, R], BF16) for i in range(2)]
        spread_bf = [kept("spread_bf%d" % k, [P, L * PACK], BF16) for k in range(2)]
        spread_codes = [kept("spread_codes%d" % k, [P, L], U32) for k in range(2)]
        spread_scales = [kept("spread_scales%d" % k, [P, L], U8) for k in range(2)]
        d_raw = kept("d_raw", [P, 2, 2 * L], U8)
        d_codes = kept("d_codes", [P, 2, 2 * L], U8)
        ds_raw = kept("ds_raw", [P, 2, L], U8)
        ds_plane = kept("ds_plane", [P, 2, L], U8)
        x_codes = [kept("x_codes%d" % h, [P, 2, WIDE], U32) for h in range(2)]
        xs_plane = kept("xs_plane", [P, 2, M], U8)
        first_raw = [kept("first_raw%d" % k, [P, PACK, WIDE], BF16) for k in range(2)]
        waves_raw = {g: kept("waves_raw%d" % g, [P, 2, PACK, WIDE], BF16) for g in range(1, CHUNKS)}
        waves_codes = [kept("waves_codes%d" % g, [P, 2 * WIDE], U32) for g in range(CHUNKS)]
        waves_scales = [kept("waves_scales%d" % g, [P, 2 * WIDE], U8) for g in range(CHUNKS)]
        taps_bf = [kept("taps_bf%d" % h, [P, PACK, WIDE], BF16) for h in range(2)]
        shrunk_codes = [kept("shrunk_codes%d" % h, [P, WIDE], U32) for h in range(2)]
        shrunk_scales = [kept("shrunk_scales%d" % h, [P, WIDE], U8) for h in range(2)]
        c_bf = [kept("c_bf%d" % g, [P, WIDE * PACK], BF16) for g in range(CHUNKS)]
        c_codes = [kept("c_codes%d" % g, [P, WIDE], U32) for g in range(CHUNKS)]
        c_scales = [kept("c_scales%d" % g, [P, WIDE], U8) for g in range(CHUNKS)]
        y_codes = {(g, h): kept("y_codes%d%d" % (g, h), [P, WIDE], U32) for g in range(CHUNKS) for h in range(2)}
        y_scales = kept("y_scales", [P, M], U8)

        count = {"product": 0, "turn": 0, "y_t": 0, "y_out": 0, "filled": 0, "taken": 0}

        def rotating(pool, kind, depth, shape, dtype):
            tag = "%s%d" % (kind, count[kind] % depth)
            count[kind] = count[kind] + 1
            if pool is psum:
                return psum.tile(shape, dtype, name=tag, tag=tag)
            return pool.tile(shape, dtype, name=tag, tag=tag, align_bytes=64)

        def turn_bank(shape, dtype):
            return rotating(psum, "turn", TURN_BANKS, shape, dtype)

        def load_waves(g, k):
            src = waves[K_PASS * k : K_PASS * (k + 1), wide(g)]
            dst = first_raw[k][:] if g == 0 else waves_raw[g][:, k, :, :]
            nc.sync.dma_start(out=dst, in_=src.rearrange("(p t) n -> p t n", t=PACK))

        def load_spread(i):
            src = spread.rearrange("(a p) k -> p a k", p=P)
            nc.sync.dma_start(out=spread_raw[i][:], in_=src[:, 2 * i : 2 * i + 2, :])

        def load_x(h):
            src = x_words.rearrange("k p m t -> p k (m t)")[:, :, PACK * WIDE * h : PACK * WIDE * (h + 1)]
            nc.sync.dma_start(out=x_codes[h][:].bitcast(I32), in_=src.bitcast(I32))

        def load_scale_rows(queue, plane, rows, quadrant):
            src = rows[:, 4 * quadrant : 4 * quadrant + 4, :].rearrange("k r n -> r k n")
            queue.dma_start(out=plane[32 * quadrant : 32 * quadrant + 4, :, :].bitcast(I32), in_=src.bitcast(I32))

        make_identity(nc, ident_f[:])
        nc.vector.memset(ds_raw[:].bitcast(I32), 0)
        nc.vector.memset(xs_plane[:].bitcast(I32), 0)
        nc.vector.memset(nsr_rows[:], 0.0)
        nc.vector.tensor_copy(out=ident_b[:], in_=ident_f[:])

        load_spread(0)
        load_waves(0, 0)
        load_spread(1)
        nc.sync.dma_start(out=d_raw[:].bitcast(I32), in_=d_words.rearrange("k p b -> p k b").bitcast(I32))
        nc.scalar.dma_start(out=front_col[:], in_=front[: N // 2].rearrange("(g p t) -> p g t", g=2, t=PACK))
        for quadrant in range(QUADRANTS - 1):
            load_scale_rows(nc.scalar, ds_raw, d_scales, quadrant)
        for quadrant in range(1, QUADRANTS):
            load_scale_rows(nc.gpsimd, xs_plane, x_scales, quadrant)
        load_x(0)
        load_waves(0, 1)
        load_x(1)
        load_waves(1, 0)
        nc.scalar.dma_start(
            out=nsr_rows[0:PACK, :].rearrange("s (q r) -> s q r", r=8),
            in_=nsr.rearrange("(q s r) -> s q r", s=PACK, r=8),
        )
        load_scale_rows(nc.scalar, ds_raw, d_scales, QUADRANTS - 1)
        load_scale_rows(nc.scalar, xs_plane, x_scales, 0)
        load_waves(1, 1)
        nc.sync.dma_start(out=agc_all[0][:], in_=agc[wide(0)].partition_broadcast(P))
        nc.sync.dma_start(out=los_col[:], in_=los.rearrange("(g p t) -> p g t", g=CHUNKS, t=PACK))
        nc.sync.dma_start(out=agc_all[1][:], in_=agc[wide(1)].partition_broadcast(P))
        for g in range(2, CHUNKS):
            for k in range(2):
                load_waves(g, k)
        nc.sync.dma_start(out=front_all[1][:], in_=front[N // 2 :].partition_broadcast(P))

        free = ["staging%d" % i for i in range(STAGING_TILES)]
        staged = {}
        made = set()

        def stage(key, after_last_quantise=False):
            tag = free[-1] if after_last_quantise else free[0]
            free.remove(tag)
            staged[key] = (tag, work.tile([P, WIDE * PACK], BF16, name=tag, tag=tag, align_bytes=64))

        def staged_part(key, x):
            tile = staged[key][1][:]
            return tile if x is None else tile[:, PACK * PART * x : PACK * PART * (x + 1)]

        def interleave(engine, key, rows, x=None):
            tile = staged_part(key, x)
            runs = rows.shape[1]
            if engine is nc.gpsimd:
                nc.gpsimd.tensor_scalar(
                    out=tile.rearrange("p (k m t) -> p k m t", k=runs, t=PACK),
                    in0=rows.rearrange("p k t m -> p k m t"),
                    scalar1=1.0, scalar2=0.0, op0=ALU.mult, op1=ALU.add,
                )
            else:
                dst = tile.rearrange("p (k c i t) -> p k c t i", k=runs, i=4, t=PACK)
                src = rows.rearrange("p k t (c i) -> p k c t i", i=4)
                if engine is nc.vector:
                    nc.vector.tensor_copy(out=dst, in_=src)
                else:
                    nc.scalar.copy(out=dst, in_=src)

        def quantise(key, codes, scales, x=None):
            if x is not None:
                codes, scales = codes[:, part(x)], scales[:, part(x)]
            nc.vector.quantize_mx(out=codes.bitcast(FP8X4), scales=scales, in_=staged_part(key, x))
            if x != 0:
                free.append(staged[key][0])

        def ready(operand):
            made.add(operand)
            fill()

        def one_run(rows, x=None):
            return (rows if x is None else rows[:, :, part(x)]).unsqueeze(1)

        def interleave_waves(engine, g, x, after_last_quantise=False):
            stage(("waves", g, x), after_last_quantise)
            interleave(engine, ("waves", g, x), waves_raw[g][:, :, :, part(x)])

        def quantise_waves(g, x):
            quantise(("waves", g, x), waves_codes[g][:, wide(x)], waves_scales[g][:, wide(x)])
            ready(("waves", g, x))

        def quantise_first(k, x=None):
            quantise(("first", k), waves_codes[0][:, wide(k)], waves_scales[0][:, wide(k)], x)

        def quantise_spread(k):
            nc.vector.quantize_mx(out=spread_codes[k][:].bitcast(FP8X4), scales=spread_scales[k][:], in_=spread_bf[k][:])

        def interleave_shrunk(engine, h, x=None):
            interleave(engine, ("shrunk", h), one_run(taps_bf[h][:], x), x)

        def quantise_shrunk(h):
            quantise(("shrunk", h), shrunk_codes[h][:], shrunk_scales[h][:])
            ready(("shrunk", h))

        def quantise_c(g):
            nc.vector.quantize_mx(out=c_codes[g][:].bitcast(FP8X4), scales=c_scales[g][:], in_=c_bf[g][:])
            ready(("c", g))

        y_t = {}

        def y_t_part(g, h, x):
            if g == LAST:
                return y_t[g, h, x][:]
            return y_t[g, h][:] if x is None else y_t[g, h][:, :, part(x)]

        def interleave_y(engine, g, h, x=None):
            interleave(engine, ("y", g, h), y_t_part(g, h, x).unsqueeze(1), x)

        def store_codes(g, h):
            dst = out_1[g].rearrange("p m t -> p (m t)")[:, PACK * WIDE * h : PACK * WIDE * (h + 1)]
            nc.sync.dma_start(out=dst.bitcast(I32), in_=y_codes[g, h][:].bitcast(I32))

        def quantise_y(g, h):
            quantise(("y", g, h), y_codes[g, h][:], y_scales[4 * g :, wide(h)])
            store_codes(g, h)

        def store_scales(g):
            for quadrant in range(QUADRANTS):
                first = 32 * quadrant + 4 * g
                nc.sync.dma_start(
                    out=out_2[g : g + 2, 4 * quadrant : 4 * quadrant + 4, :].bitcast(I32),
                    in_=y_scales[first : first + 8, :].bitcast(I32),
                )

        def spread_front(acc):
            for g in range(2):
                for t in range(PACK):
                    column = front_col[:, g, t : t + 1].to_broadcast([P, P])
                    nc.tensor.transpose(acc[:].bitcast(BF16)[:, block(PACK * g + t)], column, ident_b[:])

        def read_front(acc):
            nc.scalar.copy(
                out=front_all[0][:].rearrange("p (g a t) -> p g a t", g=2, t=PACK),
                in_=acc[:].bitcast(BF16).rearrange("p (g t a) -> p g a t", g=2, t=PACK),
            )

        def product_taps(acc, h, s):
            for k in range(2):
                nc.tensor.matmul_mx(
                    out=acc[:],
                    lhsT=d_codes[:, k, 2 * P * s : 2 * P * (s + 1)].bitcast(FP4X4),
                    lhsT_scale=ds_plane[:, k, block(s)],
                    rhs=x_codes[h][:, k, :].bitcast(FP8X4),
                    rhs_scale=xs_plane[:, k, wide(h)],
                    start=(k == 0), stop=(k == 1),
                )

        def read_taps(acc, h, s):
            nc.scalar.activation(out=taps_bf[h][:, s, :], in_=acc[:], func=ACT.Copy, scale=wiener[:, s : s + 1])

        def product_c(acc, g, b):
            for s in range(PACK):
                for k in range(2):
                    first = (WIDE * k + P * b) if g == 0 else (WIDE * (b // 2) + PART * k + P * (b % 2))
                    nc.tensor.matmul_mx(
                        out=acc[:, block(s)],
                        lhsT=spread_codes[k][:, block(s)].bitcast(FP8X4),
                        lhsT_scale=spread_scales[k][:, block(s)],
                        rhs=waves_codes[g][:, first : first + P].bitcast(FP8X4),
                        rhs_scale=waves_scales[g][:, first : first + P],
                        start=(k == 0), stop=(k == 1),
                    )

        def read_c(acc, g, b):
            own = slice(32 * b, 32 * (b + 1))
            gain = front_all[g // 2][:, wide(g % 2)].rearrange("p (a t) -> p a t", t=PACK)[:, own, :]
            nc.vector.tensor_tensor(
                out=c_bf[g][:].rearrange("p (t a s) -> p a s t", t=PACK, s=PACK)[:, own, :, :],
                in0=acc[:].rearrange("p (s a t) -> p a s t", s=PACK, t=PACK),
                in1=gain.unsqueeze(2).to_broadcast([P, 32, PACK, PACK]),
                op=ALU.mult,
            )

        def multiply_est(acc, g, h, t, cols):
            nc.tensor.matmul_mx(
                out=acc,
                lhsT=c_codes[g][:, block(t)].bitcast(FP8X4),
                lhsT_scale=c_scales[g][:, block(t)],
                rhs=shrunk_codes[h][:, cols].bitcast(FP8X4),
                rhs_scale=shrunk_scales[h][:, cols],
                start=True, stop=True,
            )

        def finish_y(dst, acc, g, h, t, cols):
            nc.vector.scalar_tensor_tensor(
                out=dst, in0=acc, scalar=los_col[:, g, t : t + 1], in1=agc_all[h][:, cols], op0=ALU.add, op1=ALU.mult
            )

        def product_est(acc, g, h, t):
            multiply_est(acc[:], g, h, t, wide(0))

        def read_est(acc, g, h, t):
            if t == 0:
                y_t[g, h] = rotating(work, "y_t", Y_T_TILES, [P, PACK, WIDE], F32)
            finish_y(y_t[g, h][:, t, :], acc[:], g, h, t, wide(0))

        def product_est_part(acc, h, x, pair):
            for e in range(2):
                multiply_est(acc[:, part(e)], LAST, h, 2 * pair + e, part(x))

        def read_est_part(acc, h, x, pair):
            if pair == 0:
                tag = "y_t_last%d%d" % (h, x)
                y_t[LAST, h, x] = work.tile([P, PACK, PART], F32, name=tag, tag=tag, align_bytes=64)
            for e in range(2):
                t = 2 * pair + e
                finish_y(y_t[LAST, h, x][:, t, :], acc[:, part(e)], LAST, h, t, part(x))

        def c_banks(g, banks):
            return [(product_c, read_c, (g, b), [("waves", g, b // 2), "spread"]) for b in banks]

        line = [(spread_front, read_front, (), [])]
        line.extend([(product_taps, read_taps, (0, s), ["d"]) for s in range(PACK)])
        line.extend(c_banks(0, range(4)))
        for g in range(LAST):
            for h in range(2):
                line.extend([(product_est, read_est, (g, h, t), [("c", g), ("shrunk", h)]) for t in range(PACK)])
                line.extend(c_banks(g + 1, range(2 * h, 2 * h + 2)))
        for h in range(2):
            for x in range(2):
                line.extend([(product_est_part, read_est_part, (h, x, pair), [("c", LAST)]) for pair in range(2)])
        banks = {}

        def fill():
            while count["filled"] < min(len(line), count["taken"] + PRODUCT_BANKS):
                product, reader, args, needs = line[count["filled"]]
                if not all(operand in made for operand in needs):
                    return
                acc = rotating(psum, "product", PRODUCT_BANKS, [P, WIDE], F32)
                product(acc, *args)
                banks[count["filled"]] = acc
                count["filled"] = count["filled"] + 1

        def take(n, refill=True):
            for step in range(n):
                product, reader, args, needs = line[count["taken"]]
                reader(banks[count["taken"]], *args)
                count["taken"] = count["taken"] + 1
                if refill:
                    fill()

        def turn_and_store(g, h, x):
            y_out = rotating(work, "y_out", Y_OUT_TILES, [P, 2, WIDE], F32)
            turned = []
            for j in range(2):
                tr = turn_bank([P, PACK, P], F32)
                for t in range(PACK):
                    nc.tensor.transpose(tr[:, t, :], y_t_part(g, h, x)[:, t, block(j)], ident_f[:])
                turned.append(tr)
            for j in range(2):
                nc.scalar.copy(
                    out=y_out[:, j, :].rearrange("p (a t) -> p a t", t=PACK),
                    in_=turned[j][:].rearrange("p t a -> p a t"),
                )
            first = WIDE * h + PART * x
            rows = out_0[first : first + PART, wide(g)]
            nc.sync.dma_start(out=rows.rearrange("(j p) n -> p j n", p=P), in_=y_out[:])

        fill()
        take(1)
        stage(("first", 0))
        interleave(nc.vector, ("first", 0), one_run(first_raw[0][:]))
        quantise_first(0)

        for i in range(2):
            for k in range(2):
                tr = turn_bank([P, 2, 2, P], F32)
                for u in range(2):
                    for a in range(2):
                        words = spread_raw[i][:, a, :].bitcast(F32)
                        nc.tensor.transpose(tr[:, u, a, :], words[:, 256 * k + u : 256 * (k + 1) : 2], ident_f[:])
                dst = spread_bf[k][:].bitcast(F32).rearrange("p (s i q r u) -> p s i q r u", s=PACK, i=2, q=8, r=8)
                nc.scalar.copy(
                    out=dst[:, :, i, :, :, :],
                    in_=tr[:].rearrange("p u a (c s r) -> p s (a c) r u", s=PACK, r=8),
                )
        for raw, laid in ((ds_raw, ds_plane), (d_raw, d_codes)):
            nc.vector.tensor_copy(
                out=laid[:].bitcast(I32).rearrange("p k (s q r) -> p k s q r", s=PACK, q=16),
                in_=raw[:].bitcast(I32).rearrange("p k (q s r) -> p k s q r", s=PACK, q=16),
            )
        nsr_turned = turn_bank([P, P], BF16)
        nc.tensor.transpose(nsr_turned[:], nsr_rows[:], ident_b[:])
        ready("d")
        nc.vector.tensor_scalar(out=one_plus[:], in0=nsr_turned[:, 0:PACK], scalar1=1.0, scalar2=None, op0=ALU.add)
        quantise_spread(0)
        nc.vector.reciprocal(out=wiener[:], in_=one_plus[:])
        quantise_spread(1)
        made.add("spread")
        take(PACK)

        stage(("first", 1))
        for x in range(2):
            interleave(nc.vector, ("first", 1), one_run(first_raw[1][:], x), x)
        for x in range(2):
            quantise_first(1, x)
            ready(("waves", 0, x))
        stage(("shrunk", 0), after_last_quantise=True)
        interleave_shrunk(nc.gpsimd, 0, 0)
        second_taps = []
        for s in range(PACK):
            acc = turn_bank([P, WIDE], F32)
            product_taps(acc, 1, s)
            second_taps.append(acc)
        interleave_waves(nc.scalar, 1, 0)
        take(4)
        interleave_shrunk(nc.vector, 0, 1)
        quantise_c(0)
        quantise_shrunk(0)
        quantise_waves(1, 0)
        for s in range(PACK):
            read_taps(second_taps[s], 1, s)
        interleave_waves(nc.gpsimd, 1, 1, after_last_quantise=True)
        stage(("shrunk", 1))
        interleave_shrunk(nc.scalar, 1)

        for g in range(LAST):
            waves_left = g + 2 < CHUNKS
            take(PACK)
            turn_and_store(g, 0, 0)
            turn_and_store(g, 0, 1)
            if waves_left:
                stage(("y", g, 0))
                interleave_y(nc.scalar, g, 0)
            take(2)
            if g == 0:
                quantise_shrunk(1)
            else:
                quantise_y(g - 1, 1)
            if not waves_left:
                store_scales(0)
            quantise_waves(g + 1, 1)

            if waves_left:
                interleave_waves(nc.gpsimd, g + 2, 0, after_last_quantise=True)
            else:
                stage(("y", g, 0), after_last_quantise=True)
                interleave_y(nc.gpsimd, g, 0)
            take(PACK)
            turn_and_store(g, 1, 0)
            turn_and_store(g, 1, 1)
            stage(("y", g, 1))
            interleave_y(nc.scalar, g, 1, None if waves_left else 1)
            take(2)
            quantise_c(g + 1)
            quantise_y(g, 0)
            if waves_left:
                quantise_waves(g + 2, 0)
                interleave_waves(nc.gpsimd, g + 2, 1, after_last_quantise=True)

        before = LAST - 1
        stage(("y", before, 1, 0), after_last_quantise=True)
        interleave(nc.gpsimd, ("y", before, 1, 0), one_run(y_t[before, 1][:], 0), 0)
        stage(("y", LAST, 0))
        for x in range(2):
            take(2, refill=False)
            turn_and_store(LAST, 0, x)
            fill()
            interleave_y(nc.gpsimd, LAST, 0, x)
        take(2)
        turn_and_store(LAST, 1, 0)
        take(2)
        stage(("y", LAST, 1))
        interleave_y(nc.vector, LAST, 1, 0)
        quantise(("y", before, 1, 0), y_codes[before, 1][:], y_scales[4 * before :, wide(1)], 0)
        quantise(("y", before, 1), y_codes[before, 1][:], y_scales[4 * before :, wide(1)], 1)
        store_codes(before, 1)
        turn_and_store(LAST, 1, 1)
        interleave_y(nc.vector, LAST, 1, 1)
        quantise_y(LAST, 0)
        quantise_y(LAST, 1)
        store_scales(before)
